import numpy as np, ml_dtypes
CORES = [48,51,52,55]
N = 4
BF = ml_dtypes.bfloat16
M, S, B, L, CAP, MISS, FILL, LN = 1024, 4096, 2048, 4, 320, 512, 3072, 2
def split(s):
    t = (13 * s) >> 2
    return t & (N - 1), (t >> LN) & (B - 1)
def first(c):
    k = np.ascontiguousarray(c, np.uint8).view(np.uint64); o = np.lexsort((k[:, 1], k[:, 0])); same = np.all(k[o[1:]] == k[o[:-1]], axis=1)
    m = np.ones(len(k), bool); m[o[1:][same]] = False; return m
def weights(rng, kind):
    w = 2 * rng.integers(0, 128, (8, 16)) + 1; w[:, :4] = 2 * rng.integers(64, 128, (8, 4)) + 1
    if kind == "near": return np.tile(np.repeat(np.array([109, 185]), 8), (8, 1))
    if kind == "spread": w[:, 4:] = rng.choice(np.array([1, 3, 255]), (8, 12))
    return rng.permuted(w, axis=1)
def pool(rng, n, kind):
    if kind == "spread": c = (1 + np.floor(255 * rng.random((n, 16)) ** 6)).astype(np.uint8)
    else: c = rng.integers(2, 255, (n, 16), dtype=np.uint8) if kind == "near" else rng.integers(1, 256, (n, 16), dtype=np.uint8)
    if kind != "near": c[0] = 1; c[1] = 255
    return c[first(c)]
def counts(rng, kind, top):
    cnt = np.zeros((N, N), np.int64)
    for r in range(N):
        if kind == "full":
            q = rng.permutation(N); left = M
            for e in [top] + [int(x) for x in q if x != top]:
                cnt[r, e] = min(CAP, left); left -= min(CAP, left)
        else:
            v = rng.multinomial(M, np.full(N, 2.0 ** -LN))
            while np.max(v) > CAP:
                i = np.argmax(v); e = v[i] - CAP; v[i] = CAP; v[np.argmin(v)] += e
            cnt[r] = v
    return cnt
def alter(rng, ch, wg, m):
    lift = (294 - wg).astype(np.uint8); can = ch <= 255 - lift
    u = np.flatnonzero((((13 * (ch.astype(np.int64) @ wg)) & 3) != 3) & np.any(can, axis=1))[:m // 2]
    one = ch[u]; i = np.argmax(np.where(can[u], rng.random((len(u), 16)), -1.0), axis=1); one[np.arange(len(u)), i] += lift[i]
    two = ch[:m - len(u)].copy(); a = np.arange(len(two))
    i = rng.permuted(np.tile(np.arange(8), (len(two), 1)), axis=1)[:, :2] + 8 * rng.integers(0, 2, (len(two), 1)); two[a, i[:, 0]] += 1; two[a, i[:, 1]] -= 1
    return np.concatenate([two, one])
def make(rng, kind):
    w = weights(rng, kind); chunks = np.zeros((N, 8, 16, M), np.uint8); store = np.zeros((N, 8, 16, S), np.uint8)
    head = np.zeros((N, 8, B), np.int32); follow = np.zeros((N, 8, S), np.int32); vac = np.zeros((N, 8, MISS), np.int32)
    for g in range(8):
        c = pool(rng, N * (3 * FILL // 2 + 2 * MISS), kind); own, buc = split(c.astype(np.int64) @ w[g])
        key = own * B + buc; o = np.argsort(key, kind="stable"); ks = key[o]; rk = np.zeros(len(c), np.int64); rk[o] = np.arange(len(c)) - np.searchsorted(ks, ks)
        top = int(rng.integers(0, N)); cnt = counts(rng, kind, top); parts = [[] for r in range(N)]; stored = np.zeros(len(c), bool)
        for q in range(N):
            mine = np.flatnonzero(own == q); st = mine[rk[mine] < L][:FILL]; stored[st] = True; rest = rng.permutation(mine[~stored[mine]])
            pl = rng.permutation(S - 1) + 1; at = pl[:FILL]; vac[q, g] = pl[FILL:FILL + MISS]; store[q, g][:, at] = c[st].T
            tab = np.zeros((B, L + 1), np.int64); tab[buc[st], rk[st]] = at; head[q, g] = tab[:, 0]; follow[q, g][at] = tab[buc[st], rk[st] + 1]
            n = int(np.sum(cnt[:, q])); h = rng.permutation(FILL)
            if kind == "full": m = MISS if q == top else int(rng.integers(0, MISS + 1))
            elif kind == "deep": m = 0 if (q + g) % 2 else int(rng.integers(1, MISS + 1))
            else: m = int(rng.integers(MISS // 4, MISS + 1))
            m = min(m, n)
            if kind == "deep":
                h = h[np.argsort(-rk[st[h]], kind="stable")]; rest = rest[np.argsort(-np.count_nonzero(tab, axis=1)[buc[rest]], kind="stable")]
            if kind == "near": new = alter(rng, c[st[h]], w[g], m)
            else: new = c[rest[:m]]
            both = np.concatenate([new, c[st[h[:n - m]]]]); e = np.add.accumulate(cnt[:, q])
            if kind == "full" and q == top: both = np.roll(both, CAP * int(rng.integers(0, N)), axis=0)
            else: both = rng.permutation(both)
            for r in range(N): parts[r].append(both[e[r] - cnt[r, q]:e[r]])
        for r in range(N): chunks[r, g] = rng.permutation(np.concatenate(parts[r])).T
    return {"chunks": chunks.reshape(N, 128, M).astype(np.float32).astype(BF), "store": store.reshape(N, 128, S).astype(np.float32).astype(BF), "head": head, "follow": follow, "vac": vac,
            "wt": np.broadcast_to(w.reshape(128, 1), (N, 128, 1)).astype(np.float32)}
def setup_inputs(rng):
    return make(rng, "plain")
def setup_inputs_full(rng):
    return make(rng, "full")
def setup_inputs_near(rng):
    return make(rng, "near")
def setup_inputs_deep(rng):
    return make(rng, "deep")
def setup_inputs_spread(rng):
    return make(rng, "spread")
def whole(v, lo, hi):
    return bool(np.all((v >= lo) & (v <= hi) & (v == np.floor(v))))
def check_inputs(d):
    c, s, w = [np.asarray(d[k]).astype(np.float32) for k in ("chunks", "store", "wt")]; head, follow, vac = [np.asarray(d[k]).astype(np.int64) for k in ("head", "follow", "vac")]; bad = []
    if not whole(w, 1, 255) or not np.all(2 * np.floor(w * 0.5) != w) or not np.all(w == w[:1]): bad.append("weights")
    if not whole(c, 1, 255): bad.append("symbols")
    if not whole(s, 0, 255): bad.append("store")
    for k, v in (("head", head), ("follow", follow), ("vac", vac)):
        if not whole(v, 0, S - 1): bad.append(k)
    if bad: return bad
    c = c.astype(np.int64).reshape(N, 8, 16, M); s = s.astype(np.int64).reshape(N, 8, 16, S); w = w[0].astype(np.int64).reshape(8, 16)
    full = np.all(s > 0, axis=2); empty = np.all(s == 0, axis=2)
    if not np.all(full | empty) or np.any(full[:, :, 0]): bad.append("store")
    if np.any(follow[empty] != 0): bad.append("follow of an empty place")
    for g in range(8):
        for q in range(N):
            so, sb = split(w[g] @ s[q, g]); p = head[q, g]; seen = np.zeros(S, np.int64); ok = True
            for step in range(L):
                b = np.flatnonzero(p > 0); e = p[b]; ok = ok and bool(np.all(full[q, g][e] & (so[e] == q) & (sb[e] == b)))
                seen += np.bincount(e, minlength=S); p = follow[q, g][p]
            if not ok or np.any(p != 0) or not np.array_equal(seen, full[q, g].astype(np.int64)): bad.append("chains")
            v = vac[q, g]
            if len(np.unique(v)) != MISS or np.any(v == 0) or not np.all(empty[q, g][v]): bad.append("vacant places")
        nc = c[:, g].transpose(0, 2, 1).reshape(-1, 16); sc = s[:, g].transpose(0, 2, 1).reshape(-1, 16)[full[:, g].reshape(-1)]
        own = split(nc @ w[g])[0]; m = first(np.concatenate([sc, nc])); miss = m[len(sc):]
        if not np.all(m[:len(sc)]): bad.append("stored chunks differ")
        if not np.all(first(nc)): bad.append("new chunks differ")
        for q in range(N):
            if np.max(np.count_nonzero(own.reshape(N, M) == q, axis=1)) > CAP: bad.append("chunks of a pair")
            if np.count_nonzero(miss & (own == q)) > MISS: bad.append("misses")
    return sorted(set(bad))
def reference(chunks, store, head, follow, vac, wt):
    y = np.zeros((N, 8, M), np.float32); z = np.array(store)
    for g in range(8):
        raw = np.ascontiguousarray(chunks[:, 16 * g:16 * g + 16].transpose(1, 0, 2)).reshape(16, N * M)
        c = raw.astype(np.float32).astype(np.int64); own, buc = split(wt[0, 16 * g:16 * g + 16, 0].astype(np.int64) @ c); res = np.zeros(N * M, np.int64)
        for q in range(N):
            st = store[q, 16 * g:16 * g + 16].astype(np.float32).astype(np.int64); j = np.flatnonzero(own == q); v = c[:, j]
            p = head[q, g][buc[j]].astype(np.int64); ans = np.zeros(len(j), np.int64)
            for step in range(L):
                ans = np.where((p > 0) & np.all(st[:, p] == v, axis=0), p, ans); p = follow[q, g][p].astype(np.int64)
            miss = np.flatnonzero(ans == 0); new = vac[q, g][:len(miss)].astype(np.int64)
            ans[miss] = new; z[q, 16 * g:16 * g + 16][:, new] = raw[:, j[miss]]
            res[j] = q * S + ans
        y[:, g] = res.reshape(N, M)
    return {"y": y, "z": z}

@@ -1,0 +1,382 @@
+from concourse.bass import DstId, RemoteDMATransfer
+from concourse.mybir import AluOpType as ALU, ActivationFunctionType as ACT
+
+N = 4
+M, S, B, CAP, MISS = 1024, 4096, 2048, 320, 512
+H = 2 * CAP
+HC = H // 16
+FTW = 4624
+ZWW = 5488
+BIG = 5120.0
+PS = 8192.0
+
+SCRATCH = {
+    "c0": ("sbuf", [128, M], "bfloat16"),
+    "wcol": ("sbuf", [128, 4], "float32"),
+    "cb": ("sbuf", [128, 7 * CAP], "bfloat16"),
+    "ab": ("sbuf", [128, 7 * CAP], "bfloat16"),
+    "zw": ("sbuf", [128, ZWW], "bfloat16"),
+    "ft": ("sbuf", [128, FTW], "bfloat16"),
+    "ht": ("sbuf", [128, B], "bfloat16"),
+    "wide": ("sbuf", [128, 416], "int32"),
+    "whi": ("sbuf", [128, 416], "bfloat16"),
+    "wlo": ("sbuf", [128, 416], "bfloat16"),
+    "idhi": ("sbuf", [128, 256], "bfloat16"),
+    "idlo": ("sbuf", [128, 256], "bfloat16"),
+    "ki": ("sbuf", [128, 4], "int32"),
+    "col": ("sbuf", [128, 8], "float32"),
+    "xi": ("sbuf", [128, 144], "float32"),
+    "e16": ("sbuf", [128, 128], "float32"),
+    "slotc": ("sbuf", [128, 2 * HC], "float32"),
+    "zwt": ("sbuf", [128, 144], "bfloat16"),
+    "zs": ("sbuf", [128, 144], "bfloat16"),
+    "za": ("sbuf", [128, 144], "bfloat16"),
+    "bm": ("sbuf", [128, 128], "bfloat16"),
+    "nb": ("sbuf", [128, 128], "bfloat16"),
+    "ud0": ("sbuf", [128, 128], "bfloat16"),
+    "ud": ("sbuf", [128, 128], "bfloat16"),
+    "rst": ("sbuf", [128, 256], "bfloat16"),
+    "rs2": ("sbuf", [128, 260], "bfloat16"),
+    "t13": ("sbuf", [128, 144], "int32"),
+    "tb": ("sbuf", [128, 144], "int32"),
+    "ind": ("sbuf", [128, 260], "bfloat16"),
+    "cum": ("sbuf", [128, 260], "bfloat16"),
+    "mx": ("sbuf", [128, 256], "float32"),
+    "lst": ("sbuf", [128, 64 + 14 * HC], "uint16"),
+    "pm0": ("sbuf", [128, 2 * H], "bfloat16"),
+    "pm1": ("sbuf", [128, 2 * H], "bfloat16"),
+    "inv": ("sbuf", [128, 2 * HC], "float32"),
+    "val": ("sbuf", [128, 2 * HC], "float32"),
+    "dmp": ("sbuf", [128, 2 * HC], "float32"),
+    "pk": ("sbuf", [128, 8 * HC], "float32"),
+    "wk": ("sbuf", [128, 8 * HC], "float32"),
+    "mk": ("sbuf", [128, 8 * HC], "float32"),
+    "hp": ("sbuf", [128, 2 * HC], "float32"),
+    "ix": ("sbuf", [128, 2 * HC], "float32"),
+    "tg": ("sbuf", [128, 2 * HC], "float32"),
+    "i2": ("sbuf", [128, 2 * HC], "bfloat16"),
+    "s2": ("sbuf", [128, 2 * HC], "bfloat16"),
+    "yg": ("sbuf", [128, M], "bfloat16"),
+    "yo": ("sbuf", [128, 64], "float32"),
+    "px0": ("psum", [128, 512], "float32"),
+    "px1": ("psum", [128, 512], "float32"),
+    "pa0": ("psum", [128, 512], "float32"),
+    "pa1": ("psum", [128, 512], "float32"),
+    "pb0": ("psum", [128, 512], "float32"),
+    "pb1": ("psum", [128, 512], "float32"),
+}
+SEMAPHORES = ["qg", "qv", "qa", "qp", "dwt", "dch", "dst", "dtab", "dfo", "dht", "dft", "dy", "dz",
+              "in0", "in1", "back", "sent"]
+
+
+def layout(r):
+    s0 = 2 * ((r + 1) // 2)
+    cpos = [p for p in range(7) if not s0 <= p < s0 + 3]
+    free = list(range(s0, s0 + 3))
+    spos = [cpos[r] if q == r else free.pop(0) for q in range(N)]
+    return cpos, spos
+
+
+def emit(g, T, ops):
+    queue = {"g": g, "v": g.vector, "a": g.scalar, "p": g.tensor, "s": g.sync}
+    writer, readers, bank = {}, {}, {}
+    known = {q: set() for q in queue}
+    start, waits, needed = [], [], set()
+    group = {}
+    for i, o in enumerate(ops):
+        if o["sem"]:
+            group.setdefault(o["sem"], []).append(i)
+    for i, o in enumerate(ops):
+        q = o["q"]
+        deps = set()
+        for k in o["r"]:
+            deps.update(writer.get(k, []))
+        for k in o["w"]:
+            deps.update(writer.get(k, []))
+            deps.update(readers.get(k, []))
+        for k in o["b"]:
+            deps.update(j for e, j in bank.get(k, {}).items() if e != q)
+        deps.discard(i)
+        mine = []
+        for j in sorted(deps, reverse=True):
+            if j in known[q]:
+                continue
+            mine.append(j)
+            if ops[j]["sem"]:
+                done = group[ops[j]["sem"]]
+                assert max(done) < i
+            else:
+                done = [e for e in range(j + 1) if ops[e]["q"] == ops[j]["q"] and not ops[e]["sem"]]
+                needed.add(j)
+            for e in done:
+                known[q].add(e)
+                known[q].update(start[e])
+        waits.append(mine)
+        start.append(set(known[q]) if q else set())
+        for k in o["r"]:
+            readers.setdefault(k, []).append(i)
+        for k in o["w"]:
+            writer[k] = [i]
+            readers[k] = []
+        for k in o["b"]:
+            bank.setdefault(k, {})[q] = i
+    count, value = {}, {}
+    for i, o in enumerate(ops):
+        if i in needed:
+            count[o["q"]] = count.get(o["q"], 0) + 1
+            value[i] = ("q" + o["q"], count[o["q"]])
+        elif o["sem"]:
+            value[i] = (o["sem"], sum(ops[e]["n"] for e in group[o["sem"]]))
+    for i, o in enumerate(ops):
+        if not o["q"]:
+            continue
+        e = queue[o["q"]]
+        for s, n in sorted(set(value[j] for j in waits[i])):
+            e.wait_ge(T.sem[s], n)
+        if o["f"] is None:
+            continue
+        last = o["f"](e)
+        if i in needed:
+            last.then_inc(T.sem["q" + o["q"]], 1)
+        elif o["sem"] and o["q"] != "g":
+            last.then_inc(T.sem[o["sem"]], 16)
+
+
+def rank_program(g, core, T, topo):
+    r = T.rank_of(core)
+    if r is None:
+        return
+    ops = []
+
+    def op(q, f, rd=(), wr=(), bank=(), sem=None, n=16):
+        ops.append({"q": q, "f": f, "r": list(rd), "w": list(wr), "b": list(bank), "sem": sem, "n": n})
+
+    def ts(out, in0, s1, s2, op0, op1=None):
+        if op1 is None:
+            return lambda e: e.tensor_scalar(out, in0, s1, None, op0)
+        return lambda e: e.tensor_scalar(out, in0, s1, s2, op0, op1)
+
+    def tt(out, in0, in1, o):
+        return lambda e: e.tensor_tensor(out, in0, in1, o)
+
+    def cp(out, in_):
+        return lambda e: e.tensor_copy(out, in_)
+
+    def act(out, in_, func, **kw):
+        return lambda e: e.activation(out, in_, func, **kw)
+
+    def scan(out, d0, d1, init, op1):
+        return lambda e: e.tensor_tensor_scan(out, d0, d1, init, ALU.mult, op1)
+
+    def dma(out, in_):
+        return lambda e: e.dma_start(out, in_)
+
+    def fill(ap, v):
+        return lambda e: e.memset(ap, v)
+
+    def fold(out, sel, rhs):
+        def f(e):
+            for i in range(16):
+                last = e.matmul(out, sel[:, 15 - i:143 - i], rhs(i), i == 0, i == 15)
+            return last
+        return f
+
+    def prefix(parts):
+        def f(e):
+            for out, cum, ind in parts:
+                e.matmul(out, T.bm[:], cum, True, False)
+                last = e.matmul(out, T.ud[:], ind, False, True)
+            return last
+        return f
+
+    cpos, spos = layout(r)
+    peers = [q for q in range(N) if q != r]
+    w0 = r * CAP
+    win = slice(w0, w0 + N * CAP)
+    blk = lambda p: slice(p * CAP, (p + 1) * CAP)
+    half = [slice(cpos[2 * h] * CAP, cpos[2 * h] * CAP + H) for h in range(2)]
+    hc = [slice(h * HC, (h + 1) * HC) for h in range(2)]
+    pos = T.lst[:, 0:64]
+    lst = lambda k, h, a=0, b=HC: T.lst[:, 64 + (2 * k + h) * HC + a:64 + (2 * k + h) * HC + b]
+    pm, px, pa, pb = [T.pm0, T.pm1], [T.px0, T.px1], [T.pa0, T.pa1], [T.pb0, T.pb1]
+    c16, kr, idc, scf, msa = [T.col[:, j:j + 1] for j in range(5)]
+
+    far = [q for q in peers if topo.die(T.cores[q]) != topo.die(core)]
+    masks = {}
+    for q in peers:
+        en = topo.engines(core, T.cores[q])
+        if q in far:
+            j = far.index(q)
+            pick = en[0::2][4 * j:4 * j + 4]
+        else:
+            pick = en[1::2][0:4]
+        masks[q] = sum(1 << e for e in pick)
+
+    def send(qs, src, dst, sem):
+        def f(e):
+            trs = []
+            for q in qs:
+                rid, pid, _ = topo.addr(T.cores[q])
+                trs.append(RemoteDMATransfer(dst_ids=[DstId(rid=rid, pnc=pid)], dma_engine_mask=masks[q],
+                                             remote_sem=T.sem[sem], src=src(q), dst=dst(q)))
+            return e.remote_dma_fused(trs, local_sem=T.sem.sent)
+        return f
+
+    op("s", dma(T.c0[:], T.chunks[:]), wr=["c0"], sem="dch")
+    op("a", dma(T.wcol[:, 0:1], T.wt[:]), wr=["wt"], sem="dwt")
+    op("a", dma(T.wide[:, 256:384], T.head[:]), wr=["w1"], sem="dtab")
+    op("a", dma(T.wide[:, 384:416], T.vac[:]), wr=["w2"], sem="dtab")
+    op("s", dma(T.wide[:, 0:256], T.follow[:]), wr=["w0"], sem="dfo")
+    op("s", dma(T.zw[:, 0:S], T.store[:]), wr=["zw"], sem="dst")
+
+    io = lambda out, pat, base, mult: (lambda e: e.iota(out, pat, base, mult, allow_small_or_imprecise_dtypes=True))
+    op("g", lambda e: e.iota(T.ki[:, 0:1], [[0, 1]], 0, 1), wr=["k"])
+    op("g", io(T.xi[:], [[1, 144]], -15, 0), wr=["xi"])
+    op("g", io(T.e16[:], [[16, 8], [0, 16]], 0, 0), wr=["e16"])
+    op("g", io(kr, [[0, 1]], 16 * r, 1), wr=["kr"])
+    op("v", fill(T.cb[:, win], 0.0), wr=["win"])
+    op("v", ts(T.ki[:, 1:2], T.ki[:, 0:1], 112, None, ALU.bitwise_and), rd=["k"], wr=["k112"])
+    op("v", fill(T.rst[:], 1.0), wr=["rst"])
+    op("v", cp(c16, T.ki[:, 1:2]), rd=["k112"], wr=["c16"])
+    op("v", fill(T.rs2[:], 1.0), wr=["rs2"])
+    op("v", ts(T.nb[:], T.e16[:], c16, -1.0, ALU.is_equal, ALU.mult), rd=["e16", "c16"], wr=["nb"])
+    op("v", ts(T.bm[:], T.e16[:], c16, None, ALU.is_equal), rd=["e16", "c16"], wr=["bm"])
+    op("v", fill(T.rst[:, 0::4], 0.0), wr=["rst"])
+    op("v", fill(T.rs2[:, 0::65], 0.0), wr=["rs2"])
+    op("v", ts(T.zwt[:], T.xi[:], c16, T.wcol[:, 0:1], ALU.is_equal, ALU.mult), rd=["xi", "c16", "wt"], wr=["zwt"])
+    op("v", ts(idc, kr, c16, 256.0, ALU.subtract, ALU.mult), rd=["kr", "c16"], wr=["idc"])
+    for q in range(N):
+        op("v", fill(T.ind[:, 65 * q:65 * q + 1], float(20 * (spos[q] - r))), wr=["base%d" % q])
+    op("g", lambda e: e.affine_select(T.ud0[:], T.nb[:], [[-1, 128]], ALU.is_gt, 0.0, 0, 1), rd=["nb"], wr=["ud0"])
+    op("g", io(T.idlo[:], [[1, 256]], 0, 0), wr=["idlo"])
+    op("g", lambda e: e.affine_select(T.ud[:], T.ud0[:], [[-1, 128]], ALU.not_equal, BIG, 0, 1), rd=["ud0"], wr=["ud"])
+    op("g", io(T.ft[:, 3840:FTW], [[0, FTW - 3840]], 0, 0), wr=["f3"])
+    op("g", io(T.slotc[:], [[16, 2 * HC]], S * r + S, 1), wr=["slotc"])
+    op("a", act(T.ft[:, 0:1280], T.cb[:, win], ACT.Copy), rd=["win"], wr=["f0"])
+    op("a", act(T.ht[:, 0:1280], T.ft[:, 0:1280], ACT.Copy), rd=["f0"], wr=["g0"])
+    op("a", act(T.ht[:, 1280:B], T.ft[:, 0:B - 1280], ACT.Copy), rd=["f0"], wr=["g1"])
+    op("a", act(T.ft[:, 1280:2560], T.ft[:, 0:1280], ACT.Copy), rd=["f0"], wr=["f1"])
+    op("a", act(T.ft[:, 2560:3840], T.ft[:, 0:1280], ACT.Copy), rd=["f0"], wr=["f2"])
+    op("a", act(T.idhi[:], T.idlo[:], ACT.Identity, bias=idc, scale=0.0), rd=["idlo", "idc"], wr=["idhi"])
+
+    op("v", ts(T.wide[:, 384:416], T.wide[:, 384:416], float(S * r), None, ALU.add), rd=["w2"], wr=["w2"])
+    op("v", cp(T.whi[:, 256:416], T.wide[:, 256:416]), rd=["w1", "w2"], wr=["h1"])
+    op("v", tt(T.wlo[:, 256:416], T.wide[:, 256:416], T.whi[:, 256:416], ALU.subtract), rd=["w1", "w2", "h1"], wr=["l1"])
+    op("s", dma(T.ht[0::16, :], T.whi[:, 256:384]), rd=["g0", "g1", "h1"], wr=["ht0"], sem="dht")
+    op("s", dma(T.ht[1::16, :], T.wlo[:, 256:384]), rd=["g0", "g1", "l1"], wr=["ht1"], sem="dht")
+    ht = ["ht0", "ht1"]
+
+    op("p", fold(pa[0][:, 0:64], T.zwt, lambda i: T.c0[:, i::16]), rd=["zwt", "c0"], wr=["s"], bank=["pa0"])
+    op("v", ts(T.t13[:, 0:64], pa[0][:, 0:64], 13.0, None, ALU.mult), rd=["s"], wr=["t13"], bank=["pa0"])
+    op("v", ts(T.tb[:, 0:64], T.t13[:, 0:64], 2, N - 1, ALU.arith_shift_right, ALU.bitwise_and), rd=["t13"], wr=["own"])
+    qb = [slice(65 * q + 1, 65 * q + 65) for q in range(N)]
+    for q in range(N):
+        op("v", ts(T.ind[:, qb[q]], T.tb[:, 0:64], float(q), None, ALU.is_equal), rd=["own"], wr=["ind%d" % q])
+    op("v", scan(T.cum[:], T.rs2[:], T.ind[:], 0.0, ALU.add),
+       rd=["rs2"] + ["ind%d" % q for q in range(N)] + ["base%d" % q for q in range(N)], wr=["cum"])
+    op("p", prefix([(pa[1][:, q:256:4], T.cum[:, qb[q]], T.ind[:, qb[q]]) for q in range(N)]), rd=["bm", "ud", "cum"], wr=["pre"], bank=["pa1"])
+    op("v", cp(T.whi[:, 0:256], T.wide[:, 0:256]), rd=["w0"], wr=["h0"])
+    op("v", scan(T.mx[:], T.rst[:], pa[1][:, 0:256], 0.0, ALU.max), rd=["pre", "rst"], wr=["mx"], bank=["pa1"])
+    op("v", ts(pos, T.mx[:, 3::4], -(BIG + 1.0), None, ALU.add), rd=["mx"], wr=["pos"])
+    op("v", cp(T.cb[:, win].indirect(pos), T.c0[:]), rd=["pos", "c0"], wr=["win"])
+    op("g", send(peers, lambda q: T.cb[:, blk(spos[q])], lambda q: T.cb[:, blk(layout(q)[0][r])], "in%d" % (r // 2)),
+       rd=["win"], wr=["sent0"], sem="sent", n=4 * len(peers))
+
+    op("v", tt(T.wlo[:, 0:256], T.wide[:, 0:256], T.whi[:, 0:256], ALU.subtract), rd=["w0", "h0"], wr=["l0"])
+    zero = ["f0", "f1", "f2", "f3"]
+    rows = [("a", T.ft[3::16, 0:S], T.idlo[:], "idlo"), ("a", T.ft[2::16, 0:S], T.idhi[:], "idhi"),
+            ("s", T.ft[0::16, 0:S], T.whi[:, 0:256], "h0"),
+            ("s", T.ft[2::16, S + 1:S + 1 + MISS], T.whi[:, 384:416], "h1"),
+            ("s", T.ft[3::16, S + 1:S + 1 + MISS], T.wlo[:, 384:416], "l1"),
+            ("s", T.ft[1::16, 0:S], T.wlo[:, 0:256], "l0")]
+    for j, (q, out, in_, key) in enumerate(rows):
+        op(q, dma(out, in_), rd=zero + ["g0", "g1", key], wr=["ft%d" % j], sem="dft")
+    ft = ["ft%d" % j for j in range(len(rows))]
+
+    op("v", ts(T.ki[:, 2:3], T.ki[:, 0:1], 1, 7, ALU.arith_shift_right, ALU.bitwise_and), rd=["k"], wr=["r8"])
+    op("v", ts(T.zs[:], T.xi[:], c16, None, ALU.is_equal), rd=["xi", "c16"], wr=["zs"])
+    op("v", ts(scf, T.ki[:, 2:3], 0.0, 1.0 / PS, ALU.is_equal, ALU.mult), rd=["r8"], wr=["scf"])
+    op("v", ts(msa, T.ki[:, 2:3], 1.0, None, ALU.is_equal), rd=["r8"], wr=["msa"])
+    op("v", fill(T.zw[:, S:ZWW], 0.0), wr=["spare"])
+    op("v", ts(T.za[:], T.xi[:], c16, msa, ALU.is_equal, ALU.mult), rd=["xi", "c16", "msa"], wr=["za"])
+
+    for h in range(2):
+        op(None, None, wr=["in%d" % h], sem="in%d" % h, n=4 * len([q for q in peers if q // 2 == h]))
+    ch = [["in%d" % h] + (["win"] if r // 2 == h else []) for h in range(2)]
+    tcol = [slice(64 + h * HC, 64 + (h + 1) * HC) for h in range(2)]
+    W = 4 * HC
+    for h in range(2):
+        op("p", fold(pa[h][:, 256:256 + HC], T.zwt, lambda i, h=h: T.cb[:, half[h].start + i:half[h].stop:16]),
+           rd=["zwt"] + ch[h], wr=["sb%d" % h], bank=["pa%d" % h])
+    for h in range(2):
+        op("v", ts(T.t13[:, tcol[h]], pa[h][:, 256:256 + HC], 13.0, None, ALU.mult), rd=["sb%d" % h], wr=["u%d" % h], bank=["pa%d" % h])
+        op("v", ts(T.tb[:, tcol[h]], T.t13[:, tcol[h]], 4, B - 1, ALU.arith_shift_right, ALU.bitwise_and), rd=["u%d" % h], wr=["b%d" % h])
+        op("v", cp(lst(0, h), T.tb[:, tcol[h]]), rd=["b%d" % h], wr=["l0%d" % h])
+        op("a", act(pm[h][:, CAP:H], T.ht[:].indirect(lst(0, h, HC // 2, HC)), ACT.Identity, scale=scf),
+           rd=ht + ["l0%d" % h, "scf"], wr=["pt%d" % h])
+        op("v", ts(pm[h][:, 0:CAP], T.ht[:].indirect(lst(0, h, 0, HC // 2)), scf, None, ALU.mult),
+           rd=ht + ["l0%d" % h, "scf"], wr=["ptr%d" % h])
+        op("p", fold(px[h][:, 0:W:4], T.zs, lambda i, h=h: pm[h][:, i:H:16]), rd=["zs", "ptr%d" % h, "pt%d" % h],
+           wr=["x%d" % h], bank=["px%d" % h])
+    for k in range(1, 5):
+        for h in range(2):
+            lk = "l%d%d" % (k, h)
+            op("v", ts(lst(k, h), px[h][:, k - 1:W:4], PS, None, ALU.mult), rd=["x%d" % h], wr=[lk], bank=["px%d" % h])
+            if k < 4:
+                op("a", act(pm[h][:, 0:H], T.ft[:, 0:S].indirect(lst(k, h)), ACT.Identity, scale=scf),
+                   rd=ft + [lk, "scf"], wr=["ptr%d" % h, "pt%d" % h])
+            else:
+                op("a", act(T.pk[:, h * W:(h + 1) * W], px[h][:, 0:W], ACT.Copy), rd=["x%d" % h], wr=["pk%d" % h], bank=["px%d" % h])
+                op("a", act(T.inv[:, hc[h]], pa[h][:, 256:256 + HC], ACT.Relu, bias=32768.0, scale=-32768.0),
+                   rd=["sb%d" % h], wr=["inv%d" % h], bank=["pa%d" % h])
+                op("a", act(T.val[:, hc[h]], T.inv[:, hc[h]], ACT.Relu, bias=0.5 / PS, scale=-1.0), rd=["inv%d" % h], wr=["val%d" % h])
+            op("v", tt(pm[h][:, H:2 * H], T.zw[:, 0:S].indirect(lst(k, h)), T.cb[:, half[h]], ALU.not_equal),
+               rd=["zw", lk] + ch[h], wr=["mis%d" % h])
+            if k < 4:
+                op("p", fold(px[h][:, k:2 * W + k:4], T.zs, lambda i, h=h: pm[h][:, i::16]),
+                   rd=["zs", "ptr%d" % h, "mis%d" % h], wr=["x%d" % h], bank=["px%d" % h])
+            else:
+                op("p", fold(px[h][:, W + 4:2 * W + 4:4], T.zs, lambda i, h=h: pm[h][:, H + i::16]),
+                   rd=["zs", "mis%d" % h], wr=["x%d" % h], bank=["px%d" % h])
+
+    def number(h):
+        a = slice(h * W, (h + 1) * W)
+        found = T.mk[:, h * W + 3:(h + 1) * W:4]
+        op("v", tt(T.wk[:, a], T.pk[:, a], px[h][:, W + 1:2 * W + 1], ALU.subtract), rd=["x%d" % h, "pk%d" % h], wr=["wk%d" % h], bank=["px%d" % h])
+        op("v", scan(T.mk[:, a], T.rst[:, 0:W], T.wk[:, a], 0.0, ALU.max), rd=["wk%d" % h, "rst"], wr=["m%d" % h])
+        op("v", tt(T.i2[:, hc[h]], found, T.val[:, hc[h]], ALU.is_lt), rd=["m%d" % h, "val%d" % h], wr=["i2%d" % h])
+        op("v", scan(T.s2[:, hc[h]], T.rs2[:, 1:1 + HC], T.i2[:, hc[h]], T.s2[:, HC - 1:HC] if h else 0.0, ALU.add),
+           rd=["i2%d" % h, "rs2"] + (["s20"] if h else []), wr=["s2%d" % h])
+        op("p", prefix([(pa[h][:, 320:320 + HC], T.s2[:, hc[h]], T.i2[:, hc[h]])]), rd=["bm", "ud", "s2%d" % h, "i2%d" % h],
+           wr=["q%d" % h], bank=["pa%d" % h])
+        op("v", ts(T.hp[:, hc[h]], found, PS, 1024.0, ALU.mult, ALU.add), rd=["m%d" % h], wr=["hp%d" % h])
+        op("v", tt(T.ix[:, hc[h]], pa[h][:, 320:320 + HC], T.hp[:, hc[h]], ALU.max), rd=["q%d" % h, "hp%d" % h], wr=["ix%d" % h], bank=["pa%d" % h])
+        op("v", ts(lst(5, h), T.ix[:, hc[h]], -1024.0, None, ALU.add), rd=["ix%d" % h], wr=["l5%d" % h])
+        op("a", act(T.ab[:, half[h]], T.ft[:, 0:S + 1 + MISS].indirect(lst(5, h)), ACT.Copy), rd=ft + ["l5%d" % h], wr=["ans%d" % h])
+        qs = [q for q in peers if q // 2 == h]
+        op("g", send(qs, lambda q: T.ab[:, blk(cpos[q])], lambda q: T.ab[:, blk(layout(q)[1][r])], "back"),
+           rd=["ans%d" % h], wr=["sent%d" % (h + 1)], sem="sent", n=4 * len(qs))
+
+    def place(h):
+        op("p", fold(pb[h][:, 0:HC], T.za, lambda i: T.ab[:, half[h].start + i:half[h].stop:16]), rd=["za", "ans%d" % h],
+           wr=["y%d" % h], bank=["pb%d" % h])
+        op("v", tt(T.tg[:, hc[h]], pb[h][:, 0:HC], T.dmp[:, hc[h]], ALU.max), rd=["y%d" % h, "dmp"], wr=["tg%d" % h], bank=["pb%d" % h])
+        op("v", ts(lst(6, h), T.tg[:, hc[h]], -float(S * r), None, ALU.add), rd=["tg%d" % h], wr=["l6%d" % h])
+        op("v", cp(T.zw[:, 0:ZWW].indirect(lst(6, h)), T.cb[:, half[h]]), rd=["l6%d" % h] + ch[h], wr=["zw", "spare"])
+
+    number(0)
+    number(1)
+    op("v", tt(T.dmp[:], T.inv[:], T.slotc[:], ALU.min), rd=["inv0", "inv1", "slotc"], wr=["dmp"])
+    place(0)
+    place(1)
+    op("s", dma(T.z[:], T.zw[:, 0:S]), rd=["zw"], wr=["z"], sem="dz")
+
+    op(None, None, wr=["back"], sem="back", n=4 * len(peers))
+    op("a", act(T.yg[:], T.ab[:, win].indirect(pos), ACT.Copy), rd=["back", "pos", "ans%d" % (r // 2)], wr=["yg"])
+    op("p", fold(pa[0][:, 384:448], T.za, lambda i: T.yg[:, 64 * i:64 * i + 64]), rd=["za", "yg"], wr=["yp"], bank=["pa0"])
+    op("a", act(T.yo[:], pa[0][:, 384:448], ACT.Copy), rd=["yp"], wr=["yo"], bank=["pa0"])
+    op("a", dma(T.y[:], T.yo[:]), rd=["yo"], wr=["y"], sem="dy")
+    op("a", None, rd=["y"])
+    op("s", None, rd=["z"])
+    op("g", None, rd=["sent0", "sent1", "sent2"])
+    emit(g, T, ops)

@@ -6,67 +6,25 @@ M, S, B, CAP, MISS = 1024, 4096, 2048, 320, 512
 H = 2 * CAP
 HC = H // 16
 FTW = 4624
-ZWW = 5488
+ZWW = 5136
 BIG = 5120.0
 PS = 8192.0
+EARLY = 1536
+HA = 96
 
-SCRATCH = {
-    "c0": ("sbuf", [128, M], "bfloat16"),
-    "wcol": ("sbuf", [128, 4], "float32"),
-    "cb": ("sbuf", [128, 7 * CAP], "bfloat16"),
-    "ab": ("sbuf", [128, 7 * CAP], "bfloat16"),
-    "zw": ("sbuf", [128, ZWW], "bfloat16"),
-    "ft": ("sbuf", [128, FTW], "bfloat16"),
-    "ht": ("sbuf", [128, B], "bfloat16"),
-    "wide": ("sbuf", [128, 416], "int32"),
-    "whi": ("sbuf", [128, 416], "bfloat16"),
-    "wlo": ("sbuf", [128, 416], "bfloat16"),
-    "idhi": ("sbuf", [128, 256], "bfloat16"),
-    "idlo": ("sbuf", [128, 256], "bfloat16"),
-    "ki": ("sbuf", [128, 4], "int32"),
-    "col": ("sbuf", [128, 8], "float32"),
-    "xi": ("sbuf", [128, 144], "float32"),
-    "e16": ("sbuf", [128, 128], "float32"),
-    "slotc": ("sbuf", [128, 2 * HC], "float32"),
-    "zwt": ("sbuf", [128, 144], "bfloat16"),
-    "zs": ("sbuf", [128, 144], "bfloat16"),
-    "za": ("sbuf", [128, 144], "bfloat16"),
-    "bm": ("sbuf", [128, 128], "bfloat16"),
-    "nb": ("sbuf", [128, 128], "bfloat16"),
-    "ud0": ("sbuf", [128, 128], "bfloat16"),
-    "ud": ("sbuf", [128, 128], "bfloat16"),
-    "rst": ("sbuf", [128, 256], "bfloat16"),
-    "rs2": ("sbuf", [128, 260], "bfloat16"),
-    "t13": ("sbuf", [128, 144], "int32"),
-    "tb": ("sbuf", [128, 144], "int32"),
-    "ind": ("sbuf", [128, 260], "bfloat16"),
-    "cum": ("sbuf", [128, 260], "bfloat16"),
-    "mx": ("sbuf", [128, 256], "float32"),
-    "lst": ("sbuf", [128, 64 + 14 * HC], "uint16"),
-    "pm0": ("sbuf", [128, 2 * H], "bfloat16"),
-    "pm1": ("sbuf", [128, 2 * H], "bfloat16"),
-    "inv": ("sbuf", [128, 2 * HC], "float32"),
-    "val": ("sbuf", [128, 2 * HC], "float32"),
-    "dmp": ("sbuf", [128, 2 * HC], "float32"),
-    "pk": ("sbuf", [128, 8 * HC], "float32"),
-    "wk": ("sbuf", [128, 8 * HC], "float32"),
-    "mk": ("sbuf", [128, 8 * HC], "float32"),
-    "hp": ("sbuf", [128, 2 * HC], "float32"),
-    "ix": ("sbuf", [128, 2 * HC], "float32"),
-    "tg": ("sbuf", [128, 2 * HC], "float32"),
-    "i2": ("sbuf", [128, 2 * HC], "bfloat16"),
-    "s2": ("sbuf", [128, 2 * HC], "bfloat16"),
-    "yg": ("sbuf", [128, M], "bfloat16"),
-    "yo": ("sbuf", [128, 64], "float32"),
-    "px0": ("psum", [128, 512], "float32"),
-    "px1": ("psum", [128, 512], "float32"),
-    "pa0": ("psum", [128, 512], "float32"),
-    "pa1": ("psum", [128, 512], "float32"),
-    "pb0": ("psum", [128, 512], "float32"),
-    "pb1": ("psum", [128, 512], "float32"),
-}
-SEMAPHORES = ["qg", "qv", "qa", "qp", "dwt", "dch", "dst", "dtab", "dfo", "dht", "dft", "dy", "dz",
-              "in0", "in1", "back", "sent"]
+BF, F32, I32 = "bfloat16", "float32", "int32"
+SCRATCH = {name: ("sbuf", [128, n], dtype) for name, n, dtype in [
+    ("c0", M, BF), ("wcol", 4, F32), ("cb", 7 * CAP, BF), ("ab", 7 * CAP, BF), ("zw", ZWW, BF), ("ft", FTW, BF), ("ht", B, BF),
+    ("wide", 416, I32), ("whi", 288, BF), ("wlo", 288, BF), ("idhi", 256, BF), ("idlo", 256, BF), ("ki", 4, I32), ("col", 8, F32),
+    ("xi", 144, F32), ("e16", 128, F32), ("zwt", 144, BF), ("zs", 144, BF), ("za", 144, BF), ("zf", 144, BF), ("bm", 128, BF),
+    ("nb", 128, BF), ("ud0", 128, BF), ("ud", 128, BF), ("eye", 128, BF), ("neye", 128, BF), ("dg", 128, BF), ("rst", 256, BF),
+    ("rs2", 260, BF), ("t13", 144, I32), ("tb", 144, I32), ("tc", 2 * HC, I32), ("td", 2 * HC, I32), ("ind", 260, BF),
+    ("cum", 260, BF), ("mx", 256, F32), ("lst", 64 + 14 * HC, "uint16"), ("hl", 128, "uint16"), ("pm0", 2 * H, BF),
+    ("pm1", 2 * H, BF), ("gs", 2 * H, BF), ("inv", 2 * HC, BF), ("val", 2 * HC, F32), ("dmp", 2 * HC, BF), ("pk", 8 * HC, F32),
+    ("wk", 8 * HC, F32), ("mk", 8 * HC, F32), ("hp", 2 * HC, F32), ("ix", 2 * HC, F32), ("i2", 2 * HC, BF), ("s2", 2 * HC, BF),
+    ("yg", M, BF), ("yo", 64, F32)]}
+SCRATCH.update({name: ("psum", [128, 512], F32) for name in ["px0", "px1", "pa0", "pa1", "pb0", "pb1", "pc0", "pc1"]})
+SEMAPHORES = ["qg", "qv", "qa", "qp", "dwt", "dch", "dst", "dtab", "dfo", "dft", "dy", "dz", "in0", "in1", "back", "sent"]
 
 
 def layout(r):
@@ -174,10 +132,15 @@ def rank_program(g, core, T, topo):
     def fill(ap, v):
         return lambda e: e.memset(ap, v)
 
-    def fold(out, sel, rhs):
+    def mm(out, lhs, rhs, begin, end):
+        return lambda e: e.matmul(out, lhs, rhs, begin, end)
+
+    def fold(out, sel, rhs, more=()):
         def f(e):
+            for j, (lhs, x) in enumerate(more):
+                e.matmul(out, lhs, x, j == 0, False)
             for i in range(16):
-                last = e.matmul(out, sel[:, 15 - i:143 - i], rhs(i), i == 0, i == 15)
+                last = e.matmul(out, sel[:, 15 - i:143 - i], rhs(i), i == 0 and not more, i == 15)
             return last
         return f
 
@@ -199,7 +162,7 @@ def rank_program(g, core, T, topo):
     pos = T.lst[:, 0:64]
     lst = lambda k, h, a=0, b=HC: T.lst[:, 64 + (2 * k + h) * HC + a:64 + (2 * k + h) * HC + b]
     pm, px, pa, pb = [T.pm0, T.pm1], [T.px0, T.px1], [T.pa0, T.pa1], [T.pb0, T.pb1]
-    c16, kr, idc, scf, msa = [T.col[:, j:j + 1] for j in range(5)]
+    c16, kr, idc, scf, msa, kf, dgc, msf = [T.col[:, j:j + 1] for j in range(8)]
 
     far = [q for q in peers if topo.die(T.cores[q]) != topo.die(core)]
     masks = {}
@@ -224,16 +187,18 @@ def rank_program(g, core, T, topo):
 
     op("s", dma(T.c0[:], T.chunks[:]), wr=["c0"], sem="dch")
     op("a", dma(T.wcol[:, 0:1], T.wt[:]), wr=["wt"], sem="dwt")
-    op("a", dma(T.wide[:, 256:384], T.head[:]), wr=["w1"], sem="dtab")
-    op("a", dma(T.wide[:, 384:416], T.vac[:]), wr=["w2"], sem="dtab")
-    op("s", dma(T.wide[:, 0:256], T.follow[:]), wr=["w0"], sem="dfo")
-    op("s", dma(T.zw[:, 0:S], T.store[:]), wr=["zw"], sem="dst")
+    op("a", dma(T.wide[:, 0:256], T.follow[:]), wr=["w0"], sem="dtab")
+    op("a", dma(T.wide[:, 256:288], T.vac[:]), wr=["w2"], sem="dtab")
+    op("s", dma(T.wide[:, 288:416], T.head[:]), wr=["w1"], sem="dfo")
+    op("s", dma(T.zw[:, 0:EARLY], T.store[:, 0:EARLY]), wr=["zv"], sem="dst")
 
     io = lambda out, pat, base, mult: (lambda e: e.iota(out, pat, base, mult, allow_small_or_imprecise_dtypes=True))
     op("g", lambda e: e.iota(T.ki[:, 0:1], [[0, 1]], 0, 1), wr=["k"])
-    op("g", io(T.xi[:], [[1, 144]], -15, 0), wr=["xi"])
     op("g", io(T.e16[:], [[16, 8], [0, 16]], 0, 0), wr=["e16"])
+    op("g", io(T.xi[:], [[1, 144]], -15, 0), wr=["xi"])
     op("g", io(kr, [[0, 1]], 16 * r, 1), wr=["kr"])
+    for q in range(N):
+        op("g", io(T.ind[:, 65 * q:65 * q + 1], [[0, 1]], 20 * (spos[q] - r), 0), wr=["base%d" % q])
     op("v", fill(T.cb[:, win], 0.0), wr=["win"])
     op("v", ts(T.ki[:, 1:2], T.ki[:, 0:1], 112, None, ALU.bitwise_and), rd=["k"], wr=["k112"])
     op("v", fill(T.rst[:], 1.0), wr=["rst"])
@@ -243,28 +208,29 @@ def rank_program(g, core, T, topo):
     op("v", ts(T.bm[:], T.e16[:], c16, None, ALU.is_equal), rd=["e16", "c16"], wr=["bm"])
     op("v", fill(T.rst[:, 0::4], 0.0), wr=["rst"])
     op("v", fill(T.rs2[:, 0::65], 0.0), wr=["rs2"])
-    op("v", ts(T.zwt[:], T.xi[:], c16, T.wcol[:, 0:1], ALU.is_equal, ALU.mult), rd=["xi", "c16", "wt"], wr=["zwt"])
     op("v", ts(idc, kr, c16, 256.0, ALU.subtract, ALU.mult), rd=["kr", "c16"], wr=["idc"])
-    for q in range(N):
-        op("v", fill(T.ind[:, 65 * q:65 * q + 1], float(20 * (spos[q] - r))), wr=["base%d" % q])
+    op("v", ts(T.zwt[:], T.xi[:], c16, T.wcol[:, 0:1], ALU.is_equal, ALU.mult), rd=["xi", "c16", "wt"], wr=["zwt"])
     op("g", lambda e: e.affine_select(T.ud0[:], T.nb[:], [[-1, 128]], ALU.is_gt, 0.0, 0, 1), rd=["nb"], wr=["ud0"])
     op("g", io(T.idlo[:], [[1, 256]], 0, 0), wr=["idlo"])
     op("g", lambda e: e.affine_select(T.ud[:], T.ud0[:], [[-1, 128]], ALU.not_equal, BIG, 0, 1), rd=["ud0"], wr=["ud"])
     op("g", io(T.ft[:, 3840:FTW], [[0, FTW - 3840]], 0, 0), wr=["f3"])
-    op("g", io(T.slotc[:], [[16, 2 * HC]], S * r + S, 1), wr=["slotc"])
+    op("g", io(kf, [[0, 1]], 0, 1), wr=["kf"])
     op("a", act(T.ft[:, 0:1280], T.cb[:, win], ACT.Copy), rd=["win"], wr=["f0"])
-    op("a", act(T.ht[:, 0:1280], T.ft[:, 0:1280], ACT.Copy), rd=["f0"], wr=["g0"])
-    op("a", act(T.ht[:, 1280:B], T.ft[:, 0:B - 1280], ACT.Copy), rd=["f0"], wr=["g1"])
     op("a", act(T.ft[:, 1280:2560], T.ft[:, 0:1280], ACT.Copy), rd=["f0"], wr=["f1"])
-    op("a", act(T.ft[:, 2560:3840], T.ft[:, 0:1280], ACT.Copy), rd=["f0"], wr=["f2"])
     op("a", act(T.idhi[:], T.idlo[:], ACT.Identity, bias=idc, scale=0.0), rd=["idlo", "idc"], wr=["idhi"])
+    op("a", act(T.ft[:, 2560:3840], T.ft[:, 0:1280], ACT.Copy), rd=["f0"], wr=["f2"])
 
-    op("v", ts(T.wide[:, 384:416], T.wide[:, 384:416], float(S * r), None, ALU.add), rd=["w2"], wr=["w2"])
-    op("v", cp(T.whi[:, 256:416], T.wide[:, 256:416]), rd=["w1", "w2"], wr=["h1"])
-    op("v", tt(T.wlo[:, 256:416], T.wide[:, 256:416], T.whi[:, 256:416], ALU.subtract), rd=["w1", "w2", "h1"], wr=["l1"])
-    op("s", dma(T.ht[0::16, :], T.whi[:, 256:384]), rd=["g0", "g1", "h1"], wr=["ht0"], sem="dht")
-    op("s", dma(T.ht[1::16, :], T.wlo[:, 256:384]), rd=["g0", "g1", "l1"], wr=["ht1"], sem="dht")
-    ht = ["ht0", "ht1"]
+    op("v", ts(T.wide[:, 256:288], T.wide[:, 256:288], float(S * r), None, ALU.add), rd=["w2"], wr=["w2"])
+    op("v", cp(T.whi[:], T.wide[:, 0:288]), rd=["w0", "w2"], wr=["hi"])
+    op("v", tt(T.wlo[:], T.wide[:, 0:288], T.whi[:], ALU.subtract), rd=["w0", "w2", "hi"], wr=["lo"])
+    rows = [("s", T.ft[0::16, 0:S], T.whi[:, 0:256], "hi"), ("a", T.ft[1::16, 0:S], T.wlo[:, 0:256], "lo"),
+            ("s", T.ft[3::16, 0:S], T.idlo[:], "idlo"), ("a", T.ft[2::16, 0:S], T.idhi[:], "idhi"),
+            ("s", T.ft[2::16, S + 1:S + 1 + MISS], T.whi[:, 256:288], "hi"),
+            ("a", T.ft[3::16, S + 1:S + 1 + MISS], T.wlo[:, 256:288], "lo")]
+    for j, (q, out, in_, key) in enumerate(rows):
+        op(q, dma(out, in_), rd=["f0", "f1", "f2", "f3", key], wr=["ft%d" % j], sem="dft")
+    op("s", dma(T.zw[:, EARLY:S], T.store[:, EARLY:S]), wr=["zw"], sem="dst")
+    ft = ["ft%d" % j for j in range(len(rows))]
 
     op("p", fold(pa[0][:, 0:64], T.zwt, lambda i: T.c0[:, i::16]), rd=["zwt", "c0"], wr=["s"], bank=["pa0"])
     op("v", ts(T.t13[:, 0:64], pa[0][:, 0:64], 13.0, None, ALU.mult), rd=["s"], wr=["t13"], bank=["pa0"])
@@ -275,30 +241,27 @@ def rank_program(g, core, T, topo):
     op("v", scan(T.cum[:], T.rs2[:], T.ind[:], 0.0, ALU.add),
        rd=["rs2"] + ["ind%d" % q for q in range(N)] + ["base%d" % q for q in range(N)], wr=["cum"])
     op("p", prefix([(pa[1][:, q:256:4], T.cum[:, qb[q]], T.ind[:, qb[q]]) for q in range(N)]), rd=["bm", "ud", "cum"], wr=["pre"], bank=["pa1"])
-    op("v", cp(T.whi[:, 0:256], T.wide[:, 0:256]), rd=["w0"], wr=["h0"])
+    op("v", cp(T.hl[:], T.wide[:, 288:416]), rd=["w1"], wr=["hl"])
     op("v", scan(T.mx[:], T.rst[:], pa[1][:, 0:256], 0.0, ALU.max), rd=["pre", "rst"], wr=["mx"], bank=["pa1"])
     op("v", ts(pos, T.mx[:, 3::4], -(BIG + 1.0), None, ALU.add), rd=["mx"], wr=["pos"])
     op("v", cp(T.cb[:, win].indirect(pos), T.c0[:]), rd=["pos", "c0"], wr=["win"])
     op("g", send(peers, lambda q: T.cb[:, blk(spos[q])], lambda q: T.cb[:, blk(layout(q)[0][r])], "in%d" % (r // 2)),
        rd=["win"], wr=["sent0"], sem="sent", n=4 * len(peers))
 
-    op("v", tt(T.wlo[:, 0:256], T.wide[:, 0:256], T.whi[:, 0:256], ALU.subtract), rd=["w0", "h0"], wr=["l0"])
-    zero = ["f0", "f1", "f2", "f3"]
-    rows = [("a", T.ft[3::16, 0:S], T.idlo[:], "idlo"), ("a", T.ft[2::16, 0:S], T.idhi[:], "idhi"),
-            ("s", T.ft[0::16, 0:S], T.whi[:, 0:256], "h0"),
-            ("s", T.ft[2::16, S + 1:S + 1 + MISS], T.whi[:, 384:416], "h1"),
-            ("s", T.ft[3::16, S + 1:S + 1 + MISS], T.wlo[:, 384:416], "l1"),
-            ("s", T.ft[1::16, 0:S], T.wlo[:, 0:256], "l0")]
-    for j, (q, out, in_, key) in enumerate(rows):
-        op(q, dma(out, in_), rd=zero + ["g0", "g1", key], wr=["ft%d" % j], sem="dft")
-    ft = ["ft%d" % j for j in range(len(rows))]
+    op("a", act(T.ht[:, 0:16 * HA], T.ft[:, 0:S].indirect(T.hl[:, 0:HA]), ACT.Identity, scale=1.0 / PS), rd=ft + ["hl"], wr=["ht"])
 
+    sel = lambda out, col: ts(out, T.xi[:], c16, col, ALU.is_equal, ALU.mult)
     op("v", ts(T.ki[:, 2:3], T.ki[:, 0:1], 1, 7, ALU.arith_shift_right, ALU.bitwise_and), rd=["k"], wr=["r8"])
     op("v", ts(T.zs[:], T.xi[:], c16, None, ALU.is_equal), rd=["xi", "c16"], wr=["zs"])
-    op("v", ts(scf, T.ki[:, 2:3], 0.0, 1.0 / PS, ALU.is_equal, ALU.mult), rd=["r8"], wr=["scf"])
     op("v", ts(msa, T.ki[:, 2:3], 1.0, None, ALU.is_equal), rd=["r8"], wr=["msa"])
-    op("v", fill(T.zw[:, S:ZWW], 0.0), wr=["spare"])
-    op("v", ts(T.za[:], T.xi[:], c16, msa, ALU.is_equal, ALU.mult), rd=["xi", "c16", "msa"], wr=["za"])
+    op("v", ts(msf, T.ki[:, 2:3], 0.0, None, ALU.is_equal), rd=["r8"], wr=["msf"])
+    op("v", ts(scf, T.ki[:, 2:3], 0.0, 1.0 / PS, ALU.is_equal, ALU.mult), rd=["r8"], wr=["scf"])
+    op("v", sel(T.za[:], msa), rd=["xi", "c16", "msa"], wr=["za"])
+    op("v", sel(T.zf[:], msf), rd=["xi", "c16", "msf"], wr=["zf"])
+    op("v", ts(dgc, idc, 0.25, float(S - S * r // 4), ALU.mult, ALU.add), rd=["idc"], wr=["dgc"])
+    op("v", ts(T.eye[:], T.xi[:, 15:143], kf, None, ALU.is_equal), rd=["xi", "kf"], wr=["eye"])
+    op("v", ts(T.ht[:, 16 * HA:B], T.ft[:, 0:S].indirect(T.hl[:, HA:128]), 1.0 / PS, None, ALU.mult), rd=ft + ["hl"], wr=["hu"])
+    op("g", io(T.zw[:, S:ZWW], [[0, ZWW - S]], 0, 0), wr=["spare"])
 
     for h in range(2):
         op(None, None, wr=["in%d" % h], sem="in%d" % h, n=4 * len([q for q in peers if q // 2 == h]))
@@ -310,45 +273,108 @@ def rank_program(g, core, T, topo):
            rd=["zwt"] + ch[h], wr=["sb%d" % h], bank=["pa%d" % h])
     for h in range(2):
         op("v", ts(T.t13[:, tcol[h]], pa[h][:, 256:256 + HC], 13.0, None, ALU.mult), rd=["sb%d" % h], wr=["u%d" % h], bank=["pa%d" % h])
-        op("v", ts(T.tb[:, tcol[h]], T.t13[:, tcol[h]], 4, B - 1, ALU.arith_shift_right, ALU.bitwise_and), rd=["u%d" % h], wr=["b%d" % h])
-        op("v", cp(lst(0, h), T.tb[:, tcol[h]]), rd=["b%d" % h], wr=["l0%d" % h])
-        op("a", act(pm[h][:, CAP:H], T.ht[:].indirect(lst(0, h, HC // 2, HC)), ACT.Identity, scale=scf),
-           rd=ht + ["l0%d" % h, "scf"], wr=["pt%d" % h])
-        op("v", ts(pm[h][:, 0:CAP], T.ht[:].indirect(lst(0, h, 0, HC // 2)), scf, None, ALU.mult),
-           rd=ht + ["l0%d" % h, "scf"], wr=["ptr%d" % h])
-        op("p", fold(px[h][:, 0:W:4], T.zs, lambda i, h=h: pm[h][:, i:H:16]), rd=["zs", "ptr%d" % h, "pt%d" % h],
-           wr=["x%d" % h], bank=["px%d" % h])
-    for k in range(1, 5):
-        for h in range(2):
-            lk = "l%d%d" % (k, h)
-            op("v", ts(lst(k, h), px[h][:, k - 1:W:4], PS, None, ALU.mult), rd=["x%d" % h], wr=[lk], bank=["px%d" % h])
-            if k < 4:
-                op("a", act(pm[h][:, 0:H], T.ft[:, 0:S].indirect(lst(k, h)), ACT.Identity, scale=scf),
-                   rd=ft + [lk, "scf"], wr=["ptr%d" % h, "pt%d" % h])
-            else:
-                op("a", act(T.pk[:, h * W:(h + 1) * W], px[h][:, 0:W], ACT.Copy), rd=["x%d" % h], wr=["pk%d" % h], bank=["px%d" % h])
-                op("a", act(T.inv[:, hc[h]], pa[h][:, 256:256 + HC], ACT.Relu, bias=32768.0, scale=-32768.0),
-                   rd=["sb%d" % h], wr=["inv%d" % h], bank=["pa%d" % h])
-                op("a", act(T.val[:, hc[h]], T.inv[:, hc[h]], ACT.Relu, bias=0.5 / PS, scale=-1.0), rd=["inv%d" % h], wr=["val%d" % h])
-            op("v", tt(pm[h][:, H:2 * H], T.zw[:, 0:S].indirect(lst(k, h)), T.cb[:, half[h]], ALU.not_equal),
-               rd=["zw", lk] + ch[h], wr=["mis%d" % h])
-            if k < 4:
-                op("p", fold(px[h][:, k:2 * W + k:4], T.zs, lambda i, h=h: pm[h][:, i::16]),
-                   rd=["zs", "ptr%d" % h, "mis%d" % h], wr=["x%d" % h], bank=["px%d" % h])
-            else:
-                op("p", fold(px[h][:, W + 4:2 * W + 4:4], T.zs, lambda i, h=h: pm[h][:, H + i::16]),
-                   rd=["zs", "mis%d" % h], wr=["x%d" % h], bank=["px%d" % h])
+        op("v", ts(T.tb[:, tcol[h]], T.t13[:, tcol[h]], 2032, None, ALU.bitwise_and), rd=["u%d" % h], wr=["b%d" % h])
+        op("v", ts(T.tc[:, hc[h]], T.t13[:, tcol[h]], 11, 15, ALU.arith_shift_right, ALU.bitwise_and), rd=["u%d" % h], wr=["c%d" % h])
+        op("v", tt(T.td[:, hc[h]], T.tb[:, tcol[h]], T.tc[:, hc[h]], ALU.add), rd=["b%d" % h, "c%d" % h], wr=["d%d" % h])
+        op("v", cp(lst(0, h), T.td[:, hc[h]]), rd=["d%d" % h], wr=["l0%d" % h])
+        op("a", act(pm[h][:, CAP:H], T.ht[:].indirect(lst(0, h, HC // 2, HC)), ACT.Copy), rd=["ht", "hu", "l0%d" % h], wr=["pt%d" % h])
+        op("a", act(T.inv[:, hc[h]], pa[h][:, 256:256 + HC], ACT.Relu, bias=1.0, scale=-1.0), rd=["sb%d" % h], wr=["inv%d" % h], bank=["pa%d" % h])
+        op("a", act(T.val[:, hc[h]], T.inv[:, hc[h]], ACT.Relu, bias=0.5 / PS, scale=-1.0), rd=["inv%d" % h], wr=["val%d" % h])
+        if h == 0:
+            op("a", act(T.neye[:], T.eye[:], ACT.Identity, scale=-1.0), rd=["eye"], wr=["neye"])
+            op("a", act(T.dg[:], T.eye[:], ACT.Identity, scale=dgc), rd=["eye", "dgc"], wr=["dg"])
+        op("v", cp(pm[h][:, 0:CAP], T.ht[:].indirect(lst(0, h, 0, HC // 2))), rd=["ht", "hu", "l0%d" % h], wr=["ptr%d" % h])
+        for k, s, key in ((1, T.za, "za"), (2, T.zf, "zf")):
+            op("p", fold(px[h][:, k - 1:W:4], s, lambda i, h=h: pm[h][:, i:H:16]), rd=[key, "ptr%d" % h, "pt%d" % h],
+               wr=["x%d%d" % (k, h)], bank=["px%d" % h])
+
+    def cvt(k, h):
+        op("v", ts(lst(k, h), px[h][:, k - 1:W:4], PS, -float(S * r * (k == 1)), ALU.mult, ALU.add), rd=["x%d%d" % (k, h)],
+           wr=["l%d%d" % (k, h)], bank=["px%d" % h])
+
+    def compare(k, h, at):
+        op("v", tt(pm[h][:, at:at + H], T.zw[:, 0:S].indirect(lst(k, h)), T.cb[:, half[h]], ALU.not_equal),
+           rd=["zw", "l%d%d" % (k, h)] + ch[h], wr=["mis%d" % h] if at else ["ptr%d" % h, "pt%d" % h])
+
+    def step(k, h):
+        op("a", act(pm[h][:, 0:H], T.ft[:, 0:S].indirect(lst(k + 1, h)), ACT.Identity, scale=scf),
+           rd=ft + ["l%d%d" % (k + 1, h), "scf"], wr=["ptr%d" % h, "pt%d" % h])
+        compare(k, h, H)
+        op("p", fold(px[h][:, k + 1:2 * W + k + 1:4], T.zs, lambda i: pm[h][:, i::16]),
+           rd=["zs", "ptr%d" % h, "mis%d" % h], wr=["x%d%d" % (k + 2, h), "m%d%d" % (k, h)], bank=["px%d" % h])
+
+    def last(k, h):
+        op("p", fold(px[h][:, W + k + 1:2 * W + k + 1:4], T.zs, lambda i: pm[h][:, (k - 3) * H + i:(k - 2) * H:16]),
+           rd=["zs"] + (["ptr%d" % h, "pt%d" % h] if k == 3 else ["mis%d" % h, "mit%d" % h]), wr=["m%d%d" % (k, h)], bank=["px%d" % h])
+
+    def side(h):
+        op("a", act(T.pk[:, h * W:(h + 1) * W], px[h][:, 0:W], ACT.Copy), rd=["x%d%d" % (k, h) for k in range(1, 5)],
+           wr=["pk%d" % h], bank=["px%d" % h])
+        op("a", act(T.pk[:, h * W:(h + 1) * W:4], px[h][:, 0:W:4], ACT.Identity, bias=-0.5 * r), wr=["pk%d" % h], bank=["px%d" % h])
+
+    dbank = {(3, 0): "pc0", (3, 1): "pc1", (4, 0): "pb0"}
+
+    def minus():
+        for (k, j), name in dbank.items():
+            a = half[1].start + j * CAP
+            op("p", mm(T[name][:, 0:CAP], T.neye[:], T.cb[:, a:a + CAP], True, False), rd=["neye"] + ch[1], wr=["df" + name], bank=[name])
+
+    def pick(k):
+        a, n = (k - 3) * H, 5 - k
+        op("a", act(T.gs[:, a:a + n * CAP], T.zw[:, 0:S].indirect(lst(k, 1, 0, n * HC // 2)), ACT.Copy), rd=["zw", "l%d1" % k], wr=["gs%d" % k])
+
+    def diff(k):
+        a = (k - 3) * H
+        for j in range(5 - k):
+            name = dbank[k, j]
+            op("p", mm(T[name][:, 0:CAP], T.eye[:], T.gs[:, a + j * CAP:a + (j + 1) * CAP], False, True), rd=["eye", "gs%d" % k],
+               wr=["df" + name], bank=[name])
+
+    def size(k):
+        for j in range(5 - k):
+            name, a = dbank[k, j], (k - 3) * H + j * CAP
+            op("a", act(pm[1][:, a:a + CAP], T[name][:, 0:CAP], ACT.Abs), rd=["df" + name],
+               wr=[["ptr1", "pt1"], ["mis1"]][k - 3][j:j + 1], bank=[name])
+
+    for h in range(2):
+        cvt(1, h)
+        cvt(2, h)
+        step(1, h)
+    minus()
+    for h in range(2):
+        cvt(3, h)
+        step(2, h)
+    pick(3)
+    compare(3, 0, 0)
+    diff(3)
+    cvt(4, 0)
+    cvt(4, 1)
+    side(0)
+    last(3, 0)
+    pick(4)
+    compare(4, 0, H)
+    last(4, 0)
+    diff(4)
+    side(1)
+    op("v", tt(pm[1][:, H + CAP:2 * H], T.zw[:, 0:S].indirect(lst(4, 1, HC // 2, HC)), T.cb[:, half[1].start + CAP:half[1].stop], ALU.not_equal),
+       rd=["zw", "l41", "mis1"] + ch[1], wr=["mit1"])
+    size(3)
+    last(3, 1)
+    size(4)
 
     def number(h):
         a = slice(h * W, (h + 1) * W)
         found = T.mk[:, h * W + 3:(h + 1) * W:4]
-        op("v", tt(T.wk[:, a], T.pk[:, a], px[h][:, W + 1:2 * W + 1], ALU.subtract), rd=["x%d" % h, "pk%d" % h], wr=["wk%d" % h], bank=["px%d" % h])
+        op("v", tt(T.wk[:, a], T.pk[:, a], px[h][:, W + 2:2 * W + 2], ALU.subtract),
+           rd=["pk%d" % h] + ["m%d%d" % (k, h) for k in range(1, 5)], wr=["wk%d" % h], bank=["px%d" % h])
         op("v", scan(T.mk[:, a], T.rst[:, 0:W], T.wk[:, a], 0.0, ALU.max), rd=["wk%d" % h, "rst"], wr=["m%d" % h])
         op("v", tt(T.i2[:, hc[h]], found, T.val[:, hc[h]], ALU.is_lt), rd=["m%d" % h, "val%d" % h], wr=["i2%d" % h])
         op("v", scan(T.s2[:, hc[h]], T.rs2[:, 1:1 + HC], T.i2[:, hc[h]], T.s2[:, HC - 1:HC] if h else 0.0, ALU.add),
            rd=["i2%d" % h, "rs2"] + (["s20"] if h else []), wr=["s2%d" % h])
         op("p", prefix([(pa[h][:, 320:320 + HC], T.s2[:, hc[h]], T.i2[:, hc[h]])]), rd=["bm", "ud", "s2%d" % h, "i2%d" % h],
            wr=["q%d" % h], bank=["pa%d" % h])
+        if h == 0:
+            last(4, 1)
         op("v", ts(T.hp[:, hc[h]], found, PS, 1024.0, ALU.mult, ALU.add), rd=["m%d" % h], wr=["hp%d" % h])
         op("v", tt(T.ix[:, hc[h]], pa[h][:, 320:320 + HC], T.hp[:, hc[h]], ALU.max), rd=["q%d" % h, "hp%d" % h], wr=["ix%d" % h], bank=["pa%d" % h])
         op("v", ts(lst(5, h), T.ix[:, hc[h]], -1024.0, None, ALU.add), rd=["ix%d" % h], wr=["l5%d" % h])
@@ -358,15 +384,15 @@ def rank_program(g, core, T, topo):
            rd=["ans%d" % h], wr=["sent%d" % (h + 1)], sem="sent", n=4 * len(qs))
 
     def place(h):
-        op("p", fold(pb[h][:, 0:HC], T.za, lambda i: T.ab[:, half[h].start + i:half[h].stop:16]), rd=["za", "ans%d" % h],
-           wr=["y%d" % h], bank=["pb%d" % h])
-        op("v", tt(T.tg[:, hc[h]], pb[h][:, 0:HC], T.dmp[:, hc[h]], ALU.max), rd=["y%d" % h, "dmp"], wr=["tg%d" % h], bank=["pb%d" % h])
-        op("v", ts(lst(6, h), T.tg[:, hc[h]], -float(S * r), None, ALU.add), rd=["tg%d" % h], wr=["l6%d" % h])
+        op("p", fold(pb[h][:, 384:384 + HC], T.za, lambda i: T.ab[:, half[h].start + i:half[h].stop:16],
+                     [(T.dg[:], T.inv[:, hc[h]]), (T.eye[:], T.dmp[:, hc[h]])]),
+           rd=["za", "dg", "eye", "dmp", "ans%d" % h], wr=["y%d" % h], bank=["pb%d" % h])
+        op("v", ts(lst(6, h), pb[h][:, 384:384 + HC], -float(S * r), None, ALU.add), rd=["y%d" % h], wr=["l6%d" % h], bank=["pb%d" % h])
         op("v", cp(T.zw[:, 0:ZWW].indirect(lst(6, h)), T.cb[:, half[h]]), rd=["l6%d" % h] + ch[h], wr=["zw", "spare"])
 
     number(0)
+    op("v", tt(T.dmp[:], T.inv[:], T.idlo[:, 0:2 * HC], ALU.mult), rd=["inv0", "inv1", "idlo"], wr=["dmp"])
     number(1)
-    op("v", tt(T.dmp[:], T.inv[:], T.slotc[:], ALU.min), rd=["inv0", "inv1", "slotc"], wr=["dmp"])
     place(0)
     place(1)
     op("s", dma(T.z[:], T.zw[:, 0:S]), rd=["zw"], wr=["z"], sem="dz")

@@ -3,35 +3,38 @@ from concourse.mybir import AluOpType as ALU, ActivationFunctionType as ACT
 
 N = 4
 M, S, B, CAP, MISS = 1024, 4096, 2048, 320, 512
+BC = CAP // 16
 H = 2 * CAP
 HC = H // 16
-FTW = 4624
+WC = N * BC
+FTW = S + MISS
 ZWW = 5136
 BIG = 5120.0
 PS = 8192.0
-EARLY = 1536
-HA = 96
+UN = 128.0
+EARLY = 3072
+HA = 128
 
-BF, F32, I32 = "bfloat16", "float32", "int32"
+BF, F32, I32, U16 = "bfloat16", "float32", "int32", "uint16"
 SCRATCH = {name: ("sbuf", [128, n], dtype) for name, n, dtype in [
-    ("c0", M, BF), ("wcol", 4, F32), ("cb", 7 * CAP, BF), ("ab", 7 * CAP, BF), ("zw", ZWW, BF), ("ft", FTW, BF), ("ht", B, BF),
-    ("wide", 416, I32), ("whi", 288, BF), ("wlo", 288, BF), ("idhi", 256, BF), ("idlo", 256, BF), ("ki", 4, I32), ("col", 8, F32),
-    ("xi", 144, F32), ("e16", 128, F32), ("zwt", 144, BF), ("zs", 144, BF), ("za", 144, BF), ("zf", 144, BF), ("bm", 128, BF),
-    ("nb", 128, BF), ("ud0", 128, BF), ("ud", 128, BF), ("eye", 128, BF), ("neye", 128, BF), ("dg", 128, BF), ("rst", 256, BF),
-    ("rs2", 260, BF), ("t13", 144, I32), ("tb", 144, I32), ("tc", 2 * HC, I32), ("td", 2 * HC, I32), ("ind", 260, BF),
-    ("cum", 260, BF), ("mx", 256, F32), ("lst", 64 + 14 * HC, "uint16"), ("hl", 128, "uint16"), ("pm0", 2 * H, BF),
-    ("pm1", 2 * H, BF), ("gs", 2 * H, BF), ("inv", 2 * HC, BF), ("val", 2 * HC, F32), ("dmp", 2 * HC, BF), ("pk", 8 * HC, F32),
-    ("wk", 8 * HC, F32), ("mk", 8 * HC, F32), ("hp", 2 * HC, F32), ("ix", 2 * HC, F32), ("i2", 2 * HC, BF), ("s2", 2 * HC, BF),
-    ("yg", M, BF), ("yo", 64, F32)]}
-SCRATCH.update({name: ("psum", [128, 512], F32) for name in ["px0", "px1", "pa0", "pa1", "pb0", "pb1", "pc0", "pc1"]})
-SEMAPHORES = ["qg", "qv", "qa", "qp", "dwt", "dch", "dst", "dtab", "dfo", "dft", "dy", "dz", "in0", "in1", "back", "sent"]
+    ("c0", M, BF), ("wcol", 4, F32), ("cb", 7 * CAP, BF), ("ab", 7 * CAP, BF), ("lb", 7 * BC + 4, U16), ("zw", ZWW, BF), ("ft", FTW, BF),
+    ("ht", B, BF), ("wide", 416, I32), ("whi", 288, BF), ("wlo", 288, BF), ("idhi", 256, BF), ("idlo", 256, BF), ("ki", 4, I32),
+    ("col", 8, F32), ("xi", 144, F32), ("e16", 128, F32), ("zwt", 144, BF), ("z1", 144, BF), ("zs", 144, BF), ("z2", 144, BF),
+    ("zy", 144, BF), ("za", 144, BF), ("zf", 144, BF), ("bm", 128, BF), ("ud0", 128, BF), ("ud", 128, BF), ("nud", 128, BF),
+    ("eye", 128, BF), ("neye", 128, BF), ("dg", 128, BF), ("rst", 4 * WC, BF), ("rs2", 260, BF),
+    ("t13", WC, I32), ("tb", WC, I32), ("tc", WC, I32), ("td", WC, I32), ("ind", 260, BF), ("cum", 260, BF),
+    ("mx", 256, F32), ("lst", 64 + 6 * WC, U16), ("hl", 128, U16), ("pm", 14 * H, BF), ("gs", 2 * 512, BF),
+    ("inv", WC, BF), ("dmp", WC, BF), ("pk", 4 * WC, F32), ("wk", 4 * WC, F32), ("mk", 4 * WC, F32), ("ix", WC, F32),
+    ("i2", WC, BF), ("s2", WC + 2, BF), ("yg", M, BF), ("yo", 64, F32)]}
+SCRATCH.update({name: ("psum", [128, 512], F32) for name in ["px1", "px2", "px3", "pe", "pa0", "pa1", "pd0", "pd1"]})
+SEMAPHORES = ["qg", "qv", "qa", "qp", "dwt", "dch", "dst", "dfo", "dhd", "dva", "dft", "dfv", "dy", "dz", "in", "inl", "back",
+              "sent0", "sentl", "sent"]
 
 
 def layout(r):
-    s0 = 2 * ((r + 1) // 2)
-    cpos = [p for p in range(7) if not s0 <= p < s0 + 3]
-    free = list(range(s0, s0 + 3))
-    spos = [cpos[r] if q == r else free.pop(0) for q in range(N)]
+    cpos = [(b - r) % N + 3 if r % 2 == 0 else (b - r - 1) % N for b in range(N)]
+    free = [p for p in range(7) if p not in cpos]
+    spos = [3 if q == r else free.pop(0) for q in range(N)]
     return cpos, spos
 
 
@@ -48,7 +51,7 @@ def emit(g, T, ops):
         q = o["q"]
         deps = set()
         for k in o["r"]:
-            deps.update(writer.get(k, []))
+            deps.update(writer[k])
         for k in o["w"]:
             deps.update(writer.get(k, []))
             deps.update(readers.get(k, []))
@@ -123,6 +126,9 @@ def rank_program(g, core, T, topo):
     def act(out, in_, func, **kw):
         return lambda e: e.activation(out, in_, func, **kw)
 
+    def scaled(q, out, in_, by):
+        return ts(out, in_, by, None, ALU.mult) if q == "v" else act(out, in_, ACT.Identity, scale=by)
+
     def scan(out, d0, d1, init, op1):
         return lambda e: e.tensor_tensor_scan(out, d0, d1, init, ALU.mult, op1)
 
@@ -144,25 +150,29 @@ def rank_program(g, core, T, topo):
             return last
         return f
 
-    def prefix(parts):
+    def pairs(parts):
         def f(e):
-            for out, cum, ind in parts:
-                e.matmul(out, T.bm[:], cum, True, False)
-                last = e.matmul(out, T.ud[:], ind, False, True)
+            for out, lhs0, x0, lhs1, x1 in parts:
+                e.matmul(out, lhs0[:], x0, True, False)
+                last = e.matmul(out, lhs1[:], x1, False, True)
             return last
         return f
 
     cpos, spos = layout(r)
     peers = [q for q in range(N) if q != r]
-    w0 = r * CAP
-    win = slice(w0, w0 + N * CAP)
+    w0, c0 = min(spos), min(cpos)
+    win = slice(w0 * CAP, (w0 + N) * CAP)
     blk = lambda p: slice(p * CAP, (p + 1) * CAP)
-    half = [slice(cpos[2 * h] * CAP, cpos[2 * h] * CAP + H) for h in range(2)]
-    hc = [slice(h * HC, (h + 1) * HC) for h in range(2)]
+    lblk = lambda q, p: slice(4 * (q % 2) + p * BC, 4 * (q % 2) + (p + 1) * BC)
+    slot = lambda c: c0 * CAP + 16 * c
+    column = lambda b: BC * (cpos[b] - c0)
+    half = [column(0), column(2)]
     pos = T.lst[:, 0:64]
-    lst = lambda k, h, a=0, b=HC: T.lst[:, 64 + (2 * k + h) * HC + a:64 + (2 * k + h) * HC + b]
-    pm, px, pa, pb = [T.pm0, T.pm1], [T.px0, T.px1], [T.pa0, T.pa1], [T.pb0, T.pb1]
-    c16, kr, idc, scf, msa, kf, dgc, msf = [T.col[:, j:j + 1] for j in range(8)]
+    lst = lambda k, a, b: T.lst[:, 64 + (k - 1) * WC + a:64 + (k - 1) * WC + b]
+    pa = [T.pa0, T.pa1]
+    c16, kf, idc, dgc, n16 = [T.col[:, j:j + 1] for j in range(5)]
+    own = column(r)
+    land = BC if own == 0 else 0
 
     far = [q for q in peers if topo.die(T.cores[q]) != topo.die(core)]
     masks = {}
@@ -175,234 +185,270 @@ def rank_program(g, core, T, topo):
             pick = en[1::2][0:4]
         masks[q] = sum(1 << e for e in pick)
 
-    def send(qs, src, dst, sem):
+    def send(qs, src, dst, sem, local):
         def f(e):
             trs = []
             for q in qs:
                 rid, pid, _ = topo.addr(T.cores[q])
                 trs.append(RemoteDMATransfer(dst_ids=[DstId(rid=rid, pnc=pid)], dma_engine_mask=masks[q],
                                              remote_sem=T.sem[sem], src=src(q), dst=dst(q)))
-            return e.remote_dma_fused(trs, local_sem=T.sem.sent)
+            return e.remote_dma_fused(trs, local_sem=T.sem[local])
         return f
 
-    op("s", dma(T.c0[:], T.chunks[:]), wr=["c0"], sem="dch")
     op("a", dma(T.wcol[:, 0:1], T.wt[:]), wr=["wt"], sem="dwt")
-    op("a", dma(T.wide[:, 0:256], T.follow[:]), wr=["w0"], sem="dtab")
-    op("a", dma(T.wide[:, 256:288], T.vac[:]), wr=["w2"], sem="dtab")
-    op("s", dma(T.wide[:, 288:416], T.head[:]), wr=["w1"], sem="dfo")
+    op("s", dma(T.c0[:], T.chunks[:]), wr=["c0"], sem="dch")
+    op("a", dma(T.wide[:, 0:256], T.follow[:]), wr=["w0"], sem="dfo")
+    op("s", dma(T.wide[:, 288:416], T.head[:]), wr=["w1"], sem="dhd")
+    op("s", dma(T.wide[:, 256:288], T.vac[:]), wr=["w2"], sem="dva")
     op("s", dma(T.zw[:, 0:EARLY], T.store[:, 0:EARLY]), wr=["zv"], sem="dst")
 
     io = lambda out, pat, base, mult: (lambda e: e.iota(out, pat, base, mult, allow_small_or_imprecise_dtypes=True))
+    keep = lambda out, in_, n, cmp, other, base, mult: (lambda e: e.affine_select(out, in_, [[-mult, n]], cmp, other, base, mult))
     op("g", lambda e: e.iota(T.ki[:, 0:1], [[0, 1]], 0, 1), wr=["k"])
-    op("g", io(T.e16[:], [[16, 8], [0, 16]], 0, 0), wr=["e16"])
     op("g", io(T.xi[:], [[1, 144]], -15, 0), wr=["xi"])
-    op("g", io(kr, [[0, 1]], 16 * r, 1), wr=["kr"])
-    for q in range(N):
-        op("g", io(T.ind[:, 65 * q:65 * q + 1], [[0, 1]], 20 * (spos[q] - r), 0), wr=["base%d" % q])
+    op("g", io(T.e16[:], [[16, 8], [0, 16]], 0, 0), wr=["e16"])
+    op("g", io(T.ind[:, 0::65], [[BC, N]], 0, 0), wr=["base"])
+    op("g", io(kf, [[0, 1]], 0, 1), wr=["kf"])
     op("v", fill(T.cb[:, win], 0.0), wr=["win"])
     op("v", ts(T.ki[:, 1:2], T.ki[:, 0:1], 112, None, ALU.bitwise_and), rd=["k"], wr=["k112"])
-    op("v", fill(T.rst[:], 1.0), wr=["rst"])
-    op("v", cp(c16, T.ki[:, 1:2]), rd=["k112"], wr=["c16"])
     op("v", fill(T.rs2[:], 1.0), wr=["rs2"])
-    op("v", ts(T.nb[:], T.e16[:], c16, -1.0, ALU.is_equal, ALU.mult), rd=["e16", "c16"], wr=["nb"])
-    op("v", ts(T.bm[:], T.e16[:], c16, None, ALU.is_equal), rd=["e16", "c16"], wr=["bm"])
-    op("v", fill(T.rst[:, 0::4], 0.0), wr=["rst"])
-    op("v", fill(T.rs2[:, 0::65], 0.0), wr=["rs2"])
-    op("v", ts(idc, kr, c16, 256.0, ALU.subtract, ALU.mult), rd=["kr", "c16"], wr=["idc"])
+    op("v", cp(c16, T.ki[:, 1:2]), rd=["k112"], wr=["c16"])
+    op("v", fill(T.rst[:], 1.0), wr=["rst"])
     op("v", ts(T.zwt[:], T.xi[:], c16, T.wcol[:, 0:1], ALU.is_equal, ALU.mult), rd=["xi", "c16", "wt"], wr=["zwt"])
-    op("g", lambda e: e.affine_select(T.ud0[:], T.nb[:], [[-1, 128]], ALU.is_gt, 0.0, 0, 1), rd=["nb"], wr=["ud0"])
+    op("v", ts(T.bm[:], T.e16[:], c16, None, ALU.is_equal), rd=["e16", "c16"], wr=["bm"])
+    op("v", fill(T.rs2[:, 0::65], 0.0), wr=["rs2"])
+    op("v", fill(T.rst[:, 0::4], 0.0), wr=["rst"])
+    op("g", keep(T.ud0[:], T.bm[:], 128, ALU.is_gt, 0.0, 0, -1), rd=["bm"], wr=["ud0"])
+    op("g", keep(T.ud[:], T.ud0[:], 128, ALU.not_equal, BIG, 0, 1), rd=["ud0"], wr=["ud"])
     op("g", io(T.idlo[:], [[1, 256]], 0, 0), wr=["idlo"])
-    op("g", lambda e: e.affine_select(T.ud[:], T.ud0[:], [[-1, 128]], ALU.not_equal, BIG, 0, 1), rd=["ud0"], wr=["ud"])
-    op("g", io(T.ft[:, 3840:FTW], [[0, FTW - 3840]], 0, 0), wr=["f3"])
-    op("g", io(kf, [[0, 1]], 0, 1), wr=["kf"])
-    op("a", act(T.ft[:, 0:1280], T.cb[:, win], ACT.Copy), rd=["win"], wr=["f0"])
-    op("a", act(T.ft[:, 1280:2560], T.ft[:, 0:1280], ACT.Copy), rd=["f0"], wr=["f1"])
+    W = N * CAP
+    op("a", act(T.ft[:, 0:W], T.cb[:, win], ACT.Identity, bias=float(S * r)), rd=["win"], wr=["f0"])
+    op("a", act(n16, c16, ACT.Identity, scale=-256.0), rd=["c16"], wr=["n16"])
+    op("a", act(T.ft[:, W:2 * W], T.ft[:, 0:W], ACT.Copy), rd=["f0"], wr=["f1"])
+    op("a", act(idc, kf, ACT.Identity, scale=256.0, bias=n16), rd=["kf", "n16"], wr=["idc"])
+    op("a", act(T.z1[:], T.zwt[:], ACT.Sign), rd=["zwt"], wr=["z1"])
+    op("a", act(T.ft[:, 2 * W:3 * W], T.ft[:, 0:W], ACT.Copy), rd=["f0"], wr=["f2"])
     op("a", act(T.idhi[:], T.idlo[:], ACT.Identity, bias=idc, scale=0.0), rd=["idlo", "idc"], wr=["idhi"])
-    op("a", act(T.ft[:, 2560:3840], T.ft[:, 0:1280], ACT.Copy), rd=["f0"], wr=["f2"])
-
-    op("v", ts(T.wide[:, 256:288], T.wide[:, 256:288], float(S * r), None, ALU.add), rd=["w2"], wr=["w2"])
-    op("v", cp(T.whi[:], T.wide[:, 0:288]), rd=["w0", "w2"], wr=["hi"])
-    op("v", tt(T.wlo[:], T.wide[:, 0:288], T.whi[:], ALU.subtract), rd=["w0", "w2", "hi"], wr=["lo"])
-    rows = [("s", T.ft[0::16, 0:S], T.whi[:, 0:256], "hi"), ("a", T.ft[1::16, 0:S], T.wlo[:, 0:256], "lo"),
-            ("s", T.ft[3::16, 0:S], T.idlo[:], "idlo"), ("a", T.ft[2::16, 0:S], T.idhi[:], "idhi"),
-            ("s", T.ft[2::16, S + 1:S + 1 + MISS], T.whi[:, 256:288], "hi"),
-            ("a", T.ft[3::16, S + 1:S + 1 + MISS], T.wlo[:, 256:288], "lo")]
-    for j, (q, out, in_, key) in enumerate(rows):
-        op(q, dma(out, in_), rd=["f0", "f1", "f2", "f3", key], wr=["ft%d" % j], sem="dft")
-    op("s", dma(T.zw[:, EARLY:S], T.store[:, EARLY:S]), wr=["zw"], sem="dst")
-    ft = ["ft%d" % j for j in range(len(rows))]
+    op("g", io(T.ft[:, 3 * W:S], [[0, S - 3 * W]], S * r, 0), wr=["f3"])
 
     op("p", fold(pa[0][:, 0:64], T.zwt, lambda i: T.c0[:, i::16]), rd=["zwt", "c0"], wr=["s"], bank=["pa0"])
+    op("v", cp(T.whi[:, 0:256], T.wide[:, 0:256]), rd=["w0"], wr=["hi"])
     op("v", ts(T.t13[:, 0:64], pa[0][:, 0:64], 13.0, None, ALU.mult), rd=["s"], wr=["t13"], bank=["pa0"])
-    op("v", ts(T.tb[:, 0:64], T.t13[:, 0:64], 2, N - 1, ALU.arith_shift_right, ALU.bitwise_and), rd=["t13"], wr=["own"])
-    qb = [slice(65 * q + 1, 65 * q + 65) for q in range(N)]
-    for q in range(N):
-        op("v", ts(T.ind[:, qb[q]], T.tb[:, 0:64], float(q), None, ALU.is_equal), rd=["own"], wr=["ind%d" % q])
-    op("v", scan(T.cum[:], T.rs2[:], T.ind[:], 0.0, ALU.add),
-       rd=["rs2"] + ["ind%d" % q for q in range(N)] + ["base%d" % q for q in range(N)], wr=["cum"])
-    op("p", prefix([(pa[1][:, q:256:4], T.cum[:, qb[q]], T.ind[:, qb[q]]) for q in range(N)]), rd=["bm", "ud", "cum"], wr=["pre"], bank=["pa1"])
+    op("v", ts(T.tb[:, 0:64], T.t13[:, 0:64], 2, N - 1, ALU.arith_shift_right, ALU.bitwise_and), rd=["t13"], wr=["tb"])
+    qb = [slice(65 * j + 1, 65 * j + 65) for j in range(N)]
+    for j in range(N):
+        op("v", ts(T.ind[:, qb[j]], T.tb[:, 0:64], float(spos.index(w0 + j)), None, ALU.is_equal), rd=["tb"], wr=["ind%d" % j])
+    op("v", scan(T.cum[:], T.rs2[:], T.ind[:], 0.0, ALU.add), rd=["rs2", "base"] + ["ind%d" % j for j in range(N)], wr=["cum"])
+    op("p", pairs([(pa[1][:, j:256:4], T.bm, T.cum[:, 65 * j:65 * j + 64], T.ud, T.ind[:, qb[j]]) for j in range(N)]),
+       rd=["bm", "ud", "cum"], wr=["pre"], bank=["pa1"])
+    op("v", tt(T.wlo[:, 0:256], T.wide[:, 0:256], T.whi[:, 0:256], ALU.subtract), rd=["w0", "hi"], wr=["lo"])
+    op("v", scan(T.mx[:], T.rst[:, 0:256], pa[1][:, 0:256], 0.0, ALU.max), rd=["pre", "rst"], wr=["mx"], bank=["pa1"])
     op("v", cp(T.hl[:], T.wide[:, 288:416]), rd=["w1"], wr=["hl"])
-    op("v", scan(T.mx[:], T.rst[:], pa[1][:, 0:256], 0.0, ALU.max), rd=["pre", "rst"], wr=["mx"], bank=["pa1"])
-    op("v", ts(pos, T.mx[:, 3::4], -(BIG + 1.0), None, ALU.add), rd=["mx"], wr=["pos"])
+    op("v", ts(pos, T.mx[:, 3::4], -BIG, None, ALU.add), rd=["mx"], wr=["pos"])
     op("v", cp(T.cb[:, win].indirect(pos), T.c0[:]), rd=["pos", "c0"], wr=["win"])
-    op("g", send(peers, lambda q: T.cb[:, blk(spos[q])], lambda q: T.cb[:, blk(layout(q)[0][r])], "in%d" % (r // 2)),
-       rd=["win"], wr=["sent0"], sem="sent", n=4 * len(peers))
 
-    op("a", act(T.ht[:, 0:16 * HA], T.ft[:, 0:S].indirect(T.hl[:, 0:HA]), ACT.Identity, scale=1.0 / PS), rd=ft + ["hl"], wr=["ht"])
+    rows = [("a", T.ft[0::16, 0:S], T.whi[:, 0:256], "hi"), ("s", T.ft[1::16, 0:S], T.wlo[:, 0:256], "lo"),
+            ("s", T.ft[3::16, 0:S], T.idlo[:], "idlo"), ("a", T.ft[2::16, 0:S], T.idhi[:], "idhi")]
+    for j, (q, out, in_, key) in enumerate(rows):
+        op(q, dma(out, in_), rd=["f0", "f1", "f2", "f3", key], wr=["ft%d" % j], sem="dft")
+    op("s", dma(T.zw[:, EARLY:S], T.store[:, EARLY:S]), rd=["idhi"], wr=["zw"], sem="dst")
+    ft = ["ft%d" % j for j in range(len(rows))]
 
-    sel = lambda out, col: ts(out, T.xi[:], c16, col, ALU.is_equal, ALU.mult)
-    op("v", ts(T.ki[:, 2:3], T.ki[:, 0:1], 1, 7, ALU.arith_shift_right, ALU.bitwise_and), rd=["k"], wr=["r8"])
-    op("v", ts(T.zs[:], T.xi[:], c16, None, ALU.is_equal), rd=["xi", "c16"], wr=["zs"])
-    op("v", ts(msa, T.ki[:, 2:3], 1.0, None, ALU.is_equal), rd=["r8"], wr=["msa"])
-    op("v", ts(msf, T.ki[:, 2:3], 0.0, None, ALU.is_equal), rd=["r8"], wr=["msf"])
-    op("v", ts(scf, T.ki[:, 2:3], 0.0, 1.0 / PS, ALU.is_equal, ALU.mult), rd=["r8"], wr=["scf"])
-    op("v", sel(T.za[:], msa), rd=["xi", "c16", "msa"], wr=["za"])
-    op("v", sel(T.zf[:], msf), rd=["xi", "c16", "msf"], wr=["zf"])
-    op("v", ts(dgc, idc, 0.25, float(S - S * r // 4), ALU.mult, ALU.add), rd=["idc"], wr=["dgc"])
-    op("v", ts(T.eye[:], T.xi[:, 15:143], kf, None, ALU.is_equal), rd=["xi", "kf"], wr=["eye"])
-    op("v", ts(T.ht[:, 16 * HA:B], T.ft[:, 0:S].indirect(T.hl[:, HA:128]), 1.0 / PS, None, ALU.mult), rd=ft + ["hl"], wr=["hu"])
-    op("g", io(T.zw[:, S:ZWW], [[0, ZWW - S]], 0, 0), wr=["spare"])
+    op("a", act(T.zs[:], T.z1[:], ACT.Identity, scale=PS), rd=["z1"], wr=["zs"])
+    op("a", act(dgc, idc, ACT.Identity, scale=0.25 / UN, bias=S / UN), rd=["idc"], wr=["dgc"])
+    op("a", act(T.nud[:], T.ud[:], ACT.Identity, scale=-1.0), rd=["ud"], wr=["nud"])
+    op("g", keep(T.eye[:], T.bm[:], 128, ALU.is_equal, 0.0, 0, 1), rd=["bm"], wr=["eye"])
+    op("g", keep(T.zf[:], T.zs[:], 144, ALU.is_ge, 0.0, -14, -1), rd=["zs"], wr=["zf"])
+    op("g", keep(T.z2[:], T.zs[:], 144, ALU.is_ge, 0.0, 13, 1), rd=["zs"], wr=["z2"])
+    op("g", keep(T.za[:], T.z2[:], 144, ALU.is_ge, 0.0, -12, -1), rd=["z2"], wr=["za"])
+    op("a", act(T.neye[:], T.eye[:], ACT.Identity, scale=-1.0), rd=["eye"], wr=["neye"])
+    op("a", act(T.dg[:], T.eye[:], ACT.Identity, scale=dgc), rd=["eye", "dgc"], wr=["dg"])
 
-    for h in range(2):
-        op(None, None, wr=["in%d" % h], sem="in%d" % h, n=4 * len([q for q in peers if q // 2 == h]))
-    ch = [["in%d" % h] + (["win"] if r // 2 == h else []) for h in range(2)]
-    tcol = [slice(64 + h * HC, 64 + (h + 1) * HC) for h in range(2)]
-    W = 4 * HC
-    for h in range(2):
-        op("p", fold(pa[h][:, 256:256 + HC], T.zwt, lambda i, h=h: T.cb[:, half[h].start + i:half[h].stop:16]),
-           rd=["zwt"] + ch[h], wr=["sb%d" % h], bank=["pa%d" % h])
-    for h in range(2):
-        op("v", ts(T.t13[:, tcol[h]], pa[h][:, 256:256 + HC], 13.0, None, ALU.mult), rd=["sb%d" % h], wr=["u%d" % h], bank=["pa%d" % h])
-        op("v", ts(T.tb[:, tcol[h]], T.t13[:, tcol[h]], 2032, None, ALU.bitwise_and), rd=["u%d" % h], wr=["b%d" % h])
-        op("v", ts(T.tc[:, hc[h]], T.t13[:, tcol[h]], 11, 15, ALU.arith_shift_right, ALU.bitwise_and), rd=["u%d" % h], wr=["c%d" % h])
-        op("v", tt(T.td[:, hc[h]], T.tb[:, tcol[h]], T.tc[:, hc[h]], ALU.add), rd=["b%d" % h, "c%d" % h], wr=["d%d" % h])
-        op("v", cp(lst(0, h), T.td[:, hc[h]]), rd=["d%d" % h], wr=["l0%d" % h])
-        op("a", act(pm[h][:, CAP:H], T.ht[:].indirect(lst(0, h, HC // 2, HC)), ACT.Copy), rd=["ht", "hu", "l0%d" % h], wr=["pt%d" % h])
-        op("a", act(T.inv[:, hc[h]], pa[h][:, 256:256 + HC], ACT.Relu, bias=1.0, scale=-1.0), rd=["sb%d" % h], wr=["inv%d" % h], bank=["pa%d" % h])
-        op("a", act(T.val[:, hc[h]], T.inv[:, hc[h]], ACT.Relu, bias=0.5 / PS, scale=-1.0), rd=["inv%d" % h], wr=["val%d" % h])
-        if h == 0:
-            op("a", act(T.neye[:], T.eye[:], ACT.Identity, scale=-1.0), rd=["eye"], wr=["neye"])
-            op("a", act(T.dg[:], T.eye[:], ACT.Identity, scale=dgc), rd=["eye", "dgc"], wr=["dg"])
-        op("v", cp(pm[h][:, 0:CAP], T.ht[:].indirect(lst(0, h, 0, HC // 2))), rd=["ht", "hu", "l0%d" % h], wr=["ptr%d" % h])
-        for k, s, key in ((1, T.za, "za"), (2, T.zf, "zf")):
-            op("p", fold(px[h][:, k - 1:W:4], s, lambda i, h=h: pm[h][:, i:H:16]), rd=[key, "ptr%d" % h, "pt%d" % h],
-               wr=["x%d%d" % (k, h)], bank=["px%d" % h])
+    op("g", send(peers, lambda q: T.cb[:, blk(spos[q])], lambda q: T.cb[:, blk(layout(q)[0][r])], "in", "sent0"),
+       rd=["win"], wr=["sent0"], sem="sent0", n=4 * len(peers))
+    op("p", fold(pa[0][:, 128:128 + WC], T.zwt, lambda i: T.cb[:, win.start + i:win.stop:16]), rd=["zwt", "win"], wr=["sw"], bank=["pa0"])
+    op("v", fill(T.ft[:, S:FTW], float(S * r)), wr=["f4"])
+    op("v", cp(T.whi[:, 256:288], T.wide[:, 256:288]), rd=["w2"], wr=["vhi"])
+    op("v", fill(T.s2[:, 0:2], 64.0), wr=["s2-1"])
+    op("v", tt(T.wlo[:, 256:288], T.wide[:, 256:288], T.whi[:, 256:288], ALU.subtract), rd=["w2", "vhi"], wr=["vlo"])
+    op("v", ts(T.t13[:], pa[0][:, 128:128 + WC], 13.0, None, ALU.mult), rd=["sw"], wr=["t13"], bank=["pa0"])
+    op("v", ts(T.tb[:], T.t13[:], 2032, None, ALU.bitwise_and), rd=["t13"], wr=["tb"])
+    op("v", ts(T.tc[:], T.t13[:], 11, 15, ALU.arith_shift_right, ALU.bitwise_and), rd=["t13"], wr=["tc"])
+    op("v", tt(T.td[:], T.tb[:], T.tc[:], ALU.add), rd=["tb", "tc"], wr=["td"])
+    op("v", cp(T.lb[:, lblk(r, w0).start:lblk(r, w0 + N - 1).stop], T.td[:]), rd=["td"], wr=["lw"])
+    op("g", send(peers, lambda q: T.lb[:, lblk(r, spos[q])], lambda q: T.lb[:, lblk(q, layout(q)[0][r])], "inl", "sentl"),
+       rd=["lw"], wr=["sentL"], sem="sentl", n=4 * len(peers))
+    op("s", dma(T.ft[2::16, S:FTW], T.whi[:, 256:288]), rd=["f4", "vhi", "sentL"], wr=["fv0"], sem="dfv")
+    op("s", dma(T.ft[3::16, S:FTW], T.wlo[:, 256:288]), rd=["f4", "vlo"], wr=["fv1"], sem="dfv")
+    op("g", keep(T.zy[:], T.z2[:], 144, ALU.is_ge, 0.0, -11, -1), rd=["z2"], wr=["zy"])
+    op("v", fill(T.zw[:, S:ZWW], 0.0), wr=["spare"])
+    op(None, None, wr=["in"], sem="in", n=4 * len(peers))
+    op(None, None, wr=["inl"], sem="inl", n=4 * len(peers))
 
-    def cvt(k, h):
-        op("v", ts(lst(k, h), px[h][:, k - 1:W:4], PS, -float(S * r * (k == 1)), ALU.mult, ALU.add), rd=["x%d%d" % (k, h)],
-           wr=["l%d%d" % (k, h)], bank=["px%d" % h])
+    op("a", scaled("a", T.ht[:, 0:16 * HA], T.ft[:, 0:S].indirect(T.hl[:, 0:HA]), -1.0 / PS), rd=ft + ["hl"], wr=["ht"])
+    if HA < 128:
+        op("v", scaled("v", T.ht[:, 16 * HA:B], T.ft[:, 0:S].indirect(T.hl[:, HA:128]), -1.0 / PS), rd=ft + ["hl"], wr=["hu"])
+    ht = ["ht"] + ["hu"] * (HA < 128)
 
-    def compare(k, h, at):
-        op("v", tt(pm[h][:, at:at + H], T.zw[:, 0:S].indirect(lst(k, h)), T.cb[:, half[h]], ALU.not_equal),
-           rd=["zw", "l%d%d" % (k, h)] + ch[h], wr=["mis%d" % h] if at else ["ptr%d" % h, "pt%d" % h])
+    def span(x):
+        name, *part = str(x).split(":")
+        a, n = {"o": (own, BC), "s": (column(r ^ 1), BC), "b": (half[1 - r // 2], HC), "r": (land, 3 * BC), "w": (0, WC),
+                "0": (half[0], HC), "1": (half[1], HC)}[name]
+        return (a + int(part[0]), a + int(part[1])) if part else (a, a + n)
 
-    def step(k, h):
-        op("a", act(pm[h][:, 0:H], T.ft[:, 0:S].indirect(lst(k + 1, h)), ACT.Identity, scale=scf),
-           rd=ft + ["l%d%d" % (k + 1, h), "scf"], wr=["ptr%d" % h, "pt%d" % h])
-        compare(k, h, H)
-        op("p", fold(px[h][:, k + 1:2 * W + k + 1:4], T.zs, lambda i: pm[h][:, i::16]),
-           rd=["zs", "ptr%d" % h, "mis%d" % h], wr=["x%d%d" % (k + 2, h), "m%d%d" % (k, h)], bank=["px%d" % h])
+    keys = lambda name, a, b: ["%s.%d" % (name, c) for c in range(a // GRAIN, b // GRAIN)]
+    here = lambda a, b, mine="win", theirs="in": [mine] * (a < own + BC and b > own) + [theirs] * (a < own or b > own + BC)
+    area = lambda j, a, b: T.pm[:, 2 * H * j + 16 * a:2 * H * j + 16 * b]
+    px = lambda k, a, b: T[PX[k]][:, 128 * (k // 4) + a:128 * (k // 4) + b]
 
-    def last(k, h):
-        op("p", fold(px[h][:, W + k + 1:2 * W + k + 1:4], T.zs, lambda i: pm[h][:, (k - 3) * H + i:(k - 2) * H:16]),
-           rd=["zs"] + (["ptr%d" % h, "pt%d" % h] if k == 3 else ["mis%d" % h, "mit%d" % h]), wr=["m%d%d" % (k, h)], bank=["px%d" % h])
+    def sums():
+        op("p", fold(pa[1][:, 256 + land:256 + land + 3 * BC], T.zwt, lambda i: T.cb[:, slot(land) + i:slot(land + 3 * BC):16]),
+           rd=["zwt", "in"], wr=["sr"], bank=["pa1"])
 
-    def side(h):
-        op("a", act(T.pk[:, h * W:(h + 1) * W], px[h][:, 0:W], ACT.Copy), rd=["x%d%d" % (k, h) for k in range(1, 5)],
-           wr=["pk%d" % h], bank=["px%d" % h])
-        op("a", act(T.pk[:, h * W:(h + 1) * W:4], px[h][:, 0:W:4], ACT.Identity, bias=-0.5 * r), wr=["pk%d" % h], bank=["px%d" % h])
+    def unused(x):
+        a, b = span(x)
+        name, at = ("pa0", 128 + (3 - w0) * BC) if x == "o" else ("pa1", 256 + a)
+        op("a", act(T.inv[:, a:b], T[name][:, at:at + b - a], ACT.Relu, bias=UN, scale=-UN), rd=["sw" if x == "o" else "sr"],
+           wr=keys("inv", a, b), bank=[name])
 
-    dbank = {(3, 0): "pc0", (3, 1): "pc1", (4, 0): "pb0"}
+    def spare():
+        op("p", pairs([(pa[1][:, 400:400 + WC], T.eye, T.idlo[:, 0:WC], T.eye, T.inv[:])]), rd=["eye", "idlo"] + keys("inv", 0, WC),
+           wr=["sp"], bank=["pa1"])
+        op("a", act(T.dmp[:], pa[1][:, 400:400 + WC], ACT.Relu, bias=-UN), rd=["sp"], wr=["dmp"], bank=["pa1"])
 
-    def minus():
-        for (k, j), name in dbank.items():
-            a = half[1].start + j * CAP
-            op("p", mm(T[name][:, 0:CAP], T.neye[:], T.cb[:, a:a + CAP], True, False), rd=["neye"] + ch[1], wr=["df" + name], bank=[name])
+    def table(q, x):
+        a, b = span(x)
+        at = lblk(r, c0).start
+        out, in_ = area(0, a, b), T.ht[:].indirect(T.lb[:, at + a:at + b])
+        op(q, cp(out, in_) if q == "v" else act(out, in_, ACT.Copy), rd=ht + here(a, b, "lw", "inl"), wr=keys("t", a, b))
 
-    def pick(k):
-        a, n = (k - 3) * H, 5 - k
-        op("a", act(T.gs[:, a:a + n * CAP], T.zw[:, 0:S].indirect(lst(k, 1, 0, n * HC // 2)), ACT.Copy), rd=["zw", "l%d1" % k], wr=["gs%d" % k])
+    def follow(q, k, x):
+        a, b = span(x)
+        op(q, scaled(q, area(k - 1, a, b), T.ft[:, 0:S].indirect(lst(k, a, b)), -1.0 / PS), rd=ft + keys("l%d" % k, a, b),
+           wr=keys("p%d" % (k + 1), a, b))
 
-    def diff(k):
-        a = (k - 3) * H
-        for j in range(5 - k):
-            name = dbank[k, j]
-            op("p", mm(T[name][:, 0:CAP], T.eye[:], T.gs[:, a + j * CAP:a + (j + 1) * CAP], False, True), rd=["eye", "gs%d" % k],
-               wr=["df" + name], bank=[name])
+    def chain(k, x):
+        a, b = span(x)
+        at = 2 * H * max(k - 2, 0)
+        op("p", fold(px(k, a, b), T.za if k == 1 else T.zf, lambda i: T.pm[:, at + 16 * a + i:at + 16 * b:16]),
+           rd=["za" if k == 1 else "zf"] + keys("t" if k < 3 else "p%d" % k, a, b), wr=keys("x%d" % k, a, b), bank=[PX[k]])
 
-    def size(k):
-        for j in range(5 - k):
-            name, a = dbank[k, j], (k - 3) * H + j * CAP
-            op("a", act(pm[1][:, a:a + CAP], T[name][:, 0:CAP], ACT.Abs), rd=["df" + name],
-               wr=[["ptr1", "pt1"], ["mis1"]][k - 3][j:j + 1], bank=[name])
+    def cvt(k, x):
+        a, b = span(x)
+        op("v", ts(lst(k, a, b), px(k, a, b), -1.0, None, ALU.mult), rd=keys("x%d" % k, a, b), wr=keys("l%d" % k, a, b), bank=[PX[k]])
 
-    for h in range(2):
-        cvt(1, h)
-        cvt(2, h)
-        step(1, h)
-    minus()
-    for h in range(2):
-        cvt(3, h)
-        step(2, h)
-    pick(3)
-    compare(3, 0, 0)
-    diff(3)
-    cvt(4, 0)
-    cvt(4, 1)
-    side(0)
-    last(3, 0)
-    pick(4)
-    compare(4, 0, H)
-    last(4, 0)
-    diff(4)
-    side(1)
-    op("v", tt(pm[1][:, H + CAP:2 * H], T.zw[:, 0:S].indirect(lst(4, 1, HC // 2, HC)), T.cb[:, half[1].start + CAP:half[1].stop], ALU.not_equal),
-       rd=["zw", "l41", "mis1"] + ch[1], wr=["mit1"])
-    size(3)
-    last(3, 1)
-    size(4)
+    def compare(k, x):
+        a, b = span(x)
+        op("v", tt(area(2 + k, a, b), T.zw[:, 0:S].indirect(lst(k, a, b)), T.cb[:, slot(a):slot(b)], ALU.not_equal),
+           rd=["zw"] + keys("l%d" % k, a, b) + here(a, b), wr=keys("m%d" % k, a, b))
 
-    def number(h):
-        a = slice(h * W, (h + 1) * W)
-        found = T.mk[:, h * W + 3:(h + 1) * W:4]
-        op("v", tt(T.wk[:, a], T.pk[:, a], px[h][:, W + 2:2 * W + 2], ALU.subtract),
-           rd=["pk%d" % h] + ["m%d%d" % (k, h) for k in range(1, 5)], wr=["wk%d" % h], bank=["px%d" % h])
-        op("v", scan(T.mk[:, a], T.rst[:, 0:W], T.wk[:, a], 0.0, ALU.max), rd=["wk%d" % h, "rst"], wr=["m%d" % h])
-        op("v", tt(T.i2[:, hc[h]], found, T.val[:, hc[h]], ALU.is_lt), rd=["m%d" % h, "val%d" % h], wr=["i2%d" % h])
-        op("v", scan(T.s2[:, hc[h]], T.rs2[:, 1:1 + HC], T.i2[:, hc[h]], T.s2[:, HC - 1:HC] if h else 0.0, ALU.add),
-           rd=["i2%d" % h, "rs2"] + (["s20"] if h else []), wr=["s2%d" % h])
-        op("p", prefix([(pa[h][:, 320:320 + HC], T.s2[:, hc[h]], T.i2[:, hc[h]])]), rd=["bm", "ud", "s2%d" % h, "i2%d" % h],
-           wr=["q%d" % h], bank=["pa%d" % h])
-        if h == 0:
-            last(4, 1)
-        op("v", ts(T.hp[:, hc[h]], found, PS, 1024.0, ALU.mult, ALU.add), rd=["m%d" % h], wr=["hp%d" % h])
-        op("v", tt(T.ix[:, hc[h]], pa[h][:, 320:320 + HC], T.hp[:, hc[h]], ALU.max), rd=["q%d" % h, "hp%d" % h], wr=["ix%d" % h], bank=["pa%d" % h])
-        op("v", ts(lst(5, h), T.ix[:, hc[h]], -1024.0, None, ALU.add), rd=["ix%d" % h], wr=["l5%d" % h])
-        op("a", act(T.ab[:, half[h]], T.ft[:, 0:S + 1 + MISS].indirect(lst(5, h)), ACT.Copy), rd=ft + ["l5%d" % h], wr=["ans%d" % h])
+    def minus(j, x):
+        a, b = span(x)
+        op("p", mm(T["pd%d" % j][:, 0:16 * (b - a)], T.neye[:], T.cb[:, slot(a):slot(b)], True, False), rd=["neye"] + here(a, b),
+           wr=["df%d" % j], bank=["pd%d" % j])
+
+    def pick(j, k, x):
+        a, b = span(x)
+        op("a", act(T.gs[:, 512 * j:512 * j + 16 * (b - a)], T.zw[:, 0:S].indirect(lst(k, a, b)), ACT.Copy),
+           rd=["zw"] + keys("l%d" % k, a, b), wr=["gs%d" % j])
+
+    def plus(j, x):
+        a, b = span(x)
+        op("p", mm(T["pd%d" % j][:, 0:16 * (b - a)], T.eye[:], T.gs[:, 512 * j:512 * j + 16 * (b - a)], False, True), rd=["eye", "gs%d" % j],
+           wr=["df%d" % j], bank=["pd%d" % j])
+
+    def size(j, k, x):
+        a, b = span(x)
+        op("a", act(area(2 + k, a, b), T["pd%d" % j][:, 0:16 * (b - a)], ACT.Abs), rd=["df%d" % j], wr=keys("m%d" % k, a, b), bank=["pd%d" % j])
+
+    def differ(k, x):
+        a, b = span(x)
+        at = 2 * H * (2 + k)
+        op("p", fold(T.pe[:, 4 * a + k - 1:4 * b:4], T.zs, lambda i: T.pm[:, at + 16 * a + i:at + 16 * b:16]),
+           rd=["zs"] + keys("m%d" % k, a, b), wr=keys("e%d" % k, a, b), bank=["pe"])
+
+    def side(k, x):
+        a, b = span(x)
+        op("a", act(T.pk[:, 4 * a + k - 1:4 * b:4], px(k, a, b), ACT.Copy), rd=keys("x%d" % k, a, b), wr=keys("k%d" % k, a, b), bank=[PX[k]])
+
+    def found(x):
+        a, b = span(x)
+        c = slice(4 * a, 4 * b)
+        op("v", tt(T.wk[:, c], T.pk[:, c], T.pe[:, c], ALU.add), rd=[y for k in ("k1", "k2", "k3", "k4", "e1", "e2", "e3", "e4") for y in keys(k, a, b)],
+           wr=keys("wk", a, b), bank=["pe"])
+        op("v", scan(T.mk[:, c], T.rst[:, 0:4 * (b - a)], T.wk[:, c], 0.0, ALU.min), rd=keys("wk", a, b) + ["rst"], wr=keys("mk", a, b))
+
+    hit = lambda a, b: T.mk[:, 4 * a + 3:4 * b:4]
+
+    def missed(x):
+        a, b = span(x)
+        op("v", tt(T.i2[:, a:b], hit(a, b), T.inv[:, a:b], ALU.is_ge), rd=keys("mk", a, b) + keys("inv", a, b), wr=keys("i2", a, b))
+
+    def count(h):
+        at, (a, b) = 2 + h * HC, span(h)
+        op("v", scan(T.s2[:, at:at + HC], T.rs2[:, 1:1 + HC], T.i2[:, a:b], T.s2[:, at - 1:at], ALU.subtract),
+           rd=keys("i2", a, b) + ["rs2", "s2%d" % (h - 1)], wr=["s2%d" % h])
+
+    def rank(name, *hs):
+        op("p", pairs([(T[name][:, 400 + half[h]:400 + half[h] + HC], T.bm, T.s2[:, 1 + h * HC:1 + (h + 1) * HC], T.nud,
+                        T.i2[:, half[h]:half[h] + HC]) for h in hs]),
+           rd=["bm", "nud"] + ["s2%d" % h for h in hs], wr=[k for h in hs for k in keys("q", *span(h))], bank=[name])
+
+    def number(name, x):
+        a, b = span(x)
+        op("v", tt(T.ix[:, a:b], T[name][:, 400 + a:400 + b], hit(a, b), ALU.min), rd=keys("q", a, b), wr=keys("ix", a, b), bank=[name])
+        op("v", ts(lst(5, a, b), T.ix[:, a:b], -1.0, None, ALU.mult), rd=keys("ix", a, b), wr=keys("l5", a, b))
+
+    def answer(q, x):
+        a, b = span(x)
+        op(q, scaled(q, T.ab[:, slot(a):slot(b)], T.ft[:].indirect(lst(5, a, b)), 1.0 / PS),
+           rd=ft + ["fv0", "fv1"] + keys("l5", a, b), wr=keys("ans", a, b))
+
+    def reply(h):
         qs = [q for q in peers if q // 2 == h]
-        op("g", send(qs, lambda q: T.ab[:, blk(cpos[q])], lambda q: T.ab[:, blk(layout(q)[1][r])], "back"),
-           rd=["ans%d" % h], wr=["sent%d" % (h + 1)], sem="sent", n=4 * len(qs))
+        op("g", send(qs, lambda q: T.ab[:, blk(cpos[q])], lambda q: T.ab[:, blk(layout(q)[1][r])], "back", "sent"),
+           rd=[k for q in qs for k in keys("ans", column(q), column(q) + BC)], wr=["sent%d" % (h + 1)], sem="sent", n=4 * len(qs))
 
-    def place(h):
-        op("p", fold(pb[h][:, 384:384 + HC], T.za, lambda i: T.ab[:, half[h].start + i:half[h].stop:16],
-                     [(T.dg[:], T.inv[:, hc[h]]), (T.eye[:], T.dmp[:, hc[h]])]),
-           rd=["za", "dg", "eye", "dmp", "ans%d" % h], wr=["y%d" % h], bank=["pb%d" % h])
-        op("v", ts(lst(6, h), pb[h][:, 384:384 + HC], -float(S * r), None, ALU.add), rd=["y%d" % h], wr=["l6%d" % h], bank=["pb%d" % h])
-        op("v", cp(T.zw[:, 0:ZWW].indirect(lst(6, h)), T.cb[:, half[h]]), rd=["l6%d" % h] + ch[h], wr=["zw", "spare"])
+    def place(name, x):
+        a, b = span(x)
+        op("p", fold(T[name][:, 320 + a:320 + b], T.za, lambda i: T.ab[:, slot(a) + i:slot(b):16],
+                     [(T.dg[:], T.inv[:, a:b]), (T.eye[:], T.dmp[:, a:b])]),
+           rd=["za", "dg", "eye", "dmp"] + keys("ans", a, b), wr=keys("y", a, b), bank=[name])
 
-    number(0)
-    op("v", tt(T.dmp[:], T.inv[:], T.idlo[:, 0:2 * HC], ALU.mult), rd=["inv0", "inv1", "idlo"], wr=["dmp"])
-    number(1)
-    place(0)
-    place(1)
+    def target(name, x):
+        a, b = span(x)
+        op("v", cp(lst(6, a, b), T[name][:, 320 + a:320 + b]), rd=keys("y", a, b), wr=keys("l6", a, b), bank=[name])
+
+    def put(x):
+        a, b = span(x)
+        op("v", cp(T.zw[:].indirect(lst(6, a, b)), T.cb[:, slot(a):slot(b)]), rd=keys("l6", a, b) + here(a, b), wr=["zw", "spare"])
+
+    steps = {"sums": sums, "unused": unused, "table": table, "chain": chain, "cvt": cvt, "follow": follow, "compare": compare,
+             "minus": minus, "pick": pick, "plus": plus, "size": size, "differ": differ, "side": side, "found": found,
+             "missed": missed, "count": count, "rank": rank, "number": number, "answer": answer, "reply": reply, "spare": spare,
+             "place": place, "target": target, "put": put}
+    for line in PLAN[r // 2].split(","):
+        name, *args = line.split()
+        steps[name](*[int(x) if x.isdigit() else x for x in args])
     op("s", dma(T.z[:], T.zw[:, 0:S]), rd=["zw"], wr=["z"], sem="dz")
 
     op(None, None, wr=["back"], sem="back", n=4 * len(peers))
-    op("a", act(T.yg[:], T.ab[:, win].indirect(pos), ACT.Copy), rd=["back", "pos", "ans%d" % (r // 2)], wr=["yg"])
-    op("p", fold(pa[0][:, 384:448], T.za, lambda i: T.yg[:, 64 * i:64 * i + 64]), rd=["za", "yg"], wr=["yp"], bank=["pa0"])
-    op("a", act(T.yo[:], pa[0][:, 384:448], ACT.Copy), rd=["yp"], wr=["yo"], bank=["pa0"])
+    op("a", act(T.yg[:], T.ab[:, win].indirect(pos), ACT.Copy), rd=["back", "pos"] + keys("ans", own, own + BC), wr=["yg"])
+    op("p", fold(T.px2[:, 128:192], T.zy, lambda i: T.yg[:, 64 * i:64 * i + 64]), rd=["zy", "yg"], wr=["yp"], bank=["px2"])
+    op("a", act(T.yo[:], T.px2[:, 128:192], ACT.Copy), rd=["yp"], wr=["yo"], bank=["px2"])
     op("a", dma(T.y[:], T.yo[:]), rd=["yo"], wr=["y"], sem="dy")
     op("a", None, rd=["y"])
     op("s", None, rd=["z"])
-    op("g", None, rd=["sent0", "sent1", "sent2"])
+    op("g", None, rd=["sent0", "sentL", "sent1", "sent2"])
     emit(g, T, ops)
+
+
+GRAIN = 10
+PX = {1: "px1", 2: "px2", 3: "px3", 4: "px1"}
+PLAN = 2 * ["""sums, table v 0:0:20, table a 0:20:40, table v 1:0:20, minus 0 1:20:40, chain 2 0, unused o, table a 1:20:40, cvt 2 0, chain 1 1, chain 2 1, compare 2 0:0:40, follow a 2 0, cvt 2 1, chain 1 0, compare 2 1:0:40, cvt 1 1, chain 3 0, follow a 2 1, cvt 3 0, cvt 1 0, differ 2 w, chain 3 1, side 2 w, follow a 3 0, chain 4 0, pick 0 1 1:20:40, compare 3 0:0:40, cvt 3 1, compare 1 0:0:40, plus 0 1:20:40, differ 3 0, cvt 4 0, follow a 3 1, compare 1 1:0:20, chain 4 1, size 0 1 1:20:40, side 3 0, side 4 0, compare 4 0:0:40, side 1 w, differ 1 w, cvt 4 1, unused r, differ 4 0, minus 1 1:20:40, pick 1 3 1:20:40, plus 1 1:20:40, side 3 1, pick 0 4 1:20:40, compare 3 1:0:20, found 0, minus 0 1:20:40, size 1 3 1:20:40, side 4 1, spare, plus 0 1:20:40, missed 0, size 0 4 1:20:40, count 0, rank px3 0, differ 3 1, compare 4 1:0:20, number px3 0, differ 4 1, answer a 0:20:40, answer v 0:0:20, found 1, place pa0 0, missed 1, count 1, target pa0 0, reply 0, rank px2 1, number px2 1, answer a 1, reply 1, put 0, place pa1 1, target pa1 1, put 1"""]
+OLD = ["""unused o, table a w:40:80, table v w:0:40, chain 2 w, cvt 2 w, chain 1 w, follow a 2 w:30:80, follow v 2 w:0:30, sums, side 2 w,
+    chain 3 w, cvt 1 w, compare 2 w, minus 0 w:50:80, pick 0 1 w:50:80, unused r, side 1 w, cvt 3 w, plus 0 w:50:80, follow a 3 w:20:80, follow v 3 w:0:20,
+    differ 2 w, compare 1 w:0:50, size 0 1 w:50:80, chain 4 w, side 3 w, spare, minus 1 w:50:80, pick 1 3 w:50:80, compare 3 w:0:50, cvt 4 w,
+    differ 1 w, plus 1 w:50:80, minus 0 w:50:80, pick 0 4 w:50:80, compare 4 w:0:50, size 1 3 w:50:80, plus 0 w:50:80, side 4 w,
+    size 0 4 w:50:80, differ 3 w, differ 4 w, found w, missed w, count 0, count 1, rank px3 0 1, number px3 w, answer a 0:20:40, answer v 0:0:20,
+    answer a 1, place pa0 0, reply 0, target pa0 0, put 0, place pa1 1, reply 1, target pa1 1, put 1"""]

from concourse.bass import DstId, RemoteDMATransfer
from concourse.mybir import AluOpType as ALU, ActivationFunctionType as ACT

N = 4
M, S, B, CAP, MISS = 1024, 4096, 2048, 320, 512
BC = CAP // 16
H = 2 * CAP
HC = H // 16
WC = N * BC
FTW = S + MISS
ZWW = 5136
BIG = 5120.0
PS = 8192.0
UN = 128.0
EARLY = 3072
HA = 128

BF, F32, I32, U16 = "bfloat16", "float32", "int32", "uint16"
SCRATCH = {name: ("sbuf", [128, n], dtype) for name, n, dtype in [
    ("c0", M, BF), ("wcol", 4, F32), ("cb", 7 * CAP, BF), ("ab", 7 * CAP, BF), ("lb", 7 * BC + 4, U16), ("zw", ZWW, BF), ("ft", FTW, BF),
    ("ht", B, BF), ("wide", 416, I32), ("whi", 288, BF), ("wlo", 288, BF), ("idhi", 256, BF), ("idlo", 256, BF), ("ki", 4, I32),
    ("col", 8, F32), ("xi", 144, F32), ("e16", 128, F32), ("zwt", 144, BF), ("z1", 144, BF), ("zs", 144, BF), ("z2", 144, BF),
    ("zy", 144, BF), ("za", 144, BF), ("zf", 144, BF), ("bm", 128, BF), ("ud0", 128, BF), ("ud", 128, BF), ("nud", 128, BF),
    ("eye", 128, BF), ("neye", 128, BF), ("dg", 128, BF), ("rst", 4 * WC, BF), ("rs2", 260, BF),
    ("t13", WC, I32), ("tb", WC, I32), ("tc", WC, I32), ("td", WC, I32), ("ind", 260, BF), ("cum", 260, BF),
    ("mx", 256, F32), ("lst", 64 + 6 * WC, U16), ("hl", 128, U16), ("pm", 14 * H, BF), ("gs", 2 * 512, BF),
    ("inv", WC, BF), ("dmp", WC, BF), ("pk", 4 * WC, F32), ("wk", 4 * WC, F32), ("mk", 4 * WC, F32), ("ix", WC, F32),
    ("i2", WC, BF), ("s2", WC + 2, BF), ("yg", M, BF), ("yo", 64, F32)]}
SCRATCH.update({name: ("psum", [128, 512], F32) for name in ["px1", "px2", "px3", "pe", "pa0", "pa1", "pd0", "pd1"]})
SEMAPHORES = ["qg", "qv", "qa", "qp", "dwt", "dch", "dst", "dfo", "dhd", "dva", "dft", "dfv", "dy", "dz", "in", "inl", "back",
              "sent0", "sentl", "sent"]


def layout(r):
    cpos = [(b - r) % N + 3 if r % 2 == 0 else (b - r - 1) % N for b in range(N)]
    free = [p for p in range(7) if p not in cpos]
    spos = [3 if q == r else free.pop(0) for q in range(N)]
    return cpos, spos


def emit(g, T, ops):
    queue = {"g": g, "v": g.vector, "a": g.scalar, "p": g.tensor, "s": g.sync}
    writer, readers, bank = {}, {}, {}
    known = {q: set() for q in queue}
    start, waits, needed = [], [], set()
    group = {}
    for i, o in enumerate(ops):
        if o["sem"]:
            group.setdefault(o["sem"], []).append(i)
    for i, o in enumerate(ops):
        q = o["q"]
        deps = set()
        for k in o["r"]:
            deps.update(writer[k])
        for k in o["w"]:
            deps.update(writer.get(k, []))
            deps.update(readers.get(k, []))
        for k in o["b"]:
            deps.update(j for e, j in bank.get(k, {}).items() if e != q)
        deps.discard(i)
        mine = []
        for j in sorted(deps, reverse=True):
            if j in known[q]:
                continue
            mine.append(j)
            if ops[j]["sem"]:
                done = group[ops[j]["sem"]]
                assert max(done) < i
            else:
                done = [e for e in range(j + 1) if ops[e]["q"] == ops[j]["q"] and not ops[e]["sem"]]
                needed.add(j)
            for e in done:
                known[q].add(e)
                known[q].update(start[e])
        waits.append(mine)
        start.append(set(known[q]) if q else set())
        for k in o["r"]:
            readers.setdefault(k, []).append(i)
        for k in o["w"]:
            writer[k] = [i]
            readers[k] = []
        for k in o["b"]:
            bank.setdefault(k, {})[q] = i
    count, value = {}, {}
    for i, o in enumerate(ops):
        if i in needed:
            count[o["q"]] = count.get(o["q"], 0) + 1
            value[i] = ("q" + o["q"], count[o["q"]])
        elif o["sem"]:
            value[i] = (o["sem"], sum(ops[e]["n"] for e in group[o["sem"]]))
    for i, o in enumerate(ops):
        if not o["q"]:
            continue
        e = queue[o["q"]]
        for s, n in sorted(set(value[j] for j in waits[i])):
            e.wait_ge(T.sem[s], n)
        if o["f"] is None:
            continue
        last = o["f"](e)
        if i in needed:
            last.then_inc(T.sem["q" + o["q"]], 1)
        elif o["sem"] and o["q"] != "g":
            last.then_inc(T.sem[o["sem"]], 16)


def rank_program(g, core, T, topo):
    r = T.rank_of(core)
    if r is None:
        return
    ops = []

    def op(q, f, rd=(), wr=(), bank=(), sem=None, n=16):
        ops.append({"q": q, "f": f, "r": list(rd), "w": list(wr), "b": list(bank), "sem": sem, "n": n})

    def ts(out, in0, s1, s2, op0, op1=None):
        if op1 is None:
            return lambda e: e.tensor_scalar(out, in0, s1, None, op0)
        return lambda e: e.tensor_scalar(out, in0, s1, s2, op0, op1)

    def tt(out, in0, in1, o):
        return lambda e: e.tensor_tensor(out, in0, in1, o)

    def cp(out, in_):
        return lambda e: e.tensor_copy(out, in_)

    def act(out, in_, func, **kw):
        return lambda e: e.activation(out, in_, func, **kw)

    def scaled(q, out, in_, by):
        return ts(out, in_, by, None, ALU.mult) if q == "v" else act(out, in_, ACT.Identity, scale=by)

    def scan(out, d0, d1, init, op1):
        return lambda e: e.tensor_tensor_scan(out, d0, d1, init, ALU.mult, op1)

    def dma(out, in_):
        return lambda e: e.dma_start(out, in_)

    def fill(ap, v):
        return lambda e: e.memset(ap, v)

    def mm(out, lhs, rhs, begin, end):
        return lambda e: e.matmul(out, lhs, rhs, begin, end)

    def fold(out, sel, rhs, more=()):
        def f(e):
            for j, (lhs, x) in enumerate(more):
                e.matmul(out, lhs, x, j == 0, False)
            for i in range(16):
                last = e.matmul(out, sel[:, 15 - i:143 - i], rhs(i), i == 0 and not more, i == 15)
            return last
        return f

    def pairs(parts):
        def f(e):
            for out, lhs0, x0, lhs1, x1 in parts:
                e.matmul(out, lhs0[:], x0, True, False)
                last = e.matmul(out, lhs1[:], x1, False, True)
            return last
        return f

    cpos, spos = layout(r)
    peers = [q for q in range(N) if q != r]
    w0, c0 = min(spos), min(cpos)
    win = slice(w0 * CAP, (w0 + N) * CAP)
    blk = lambda p: slice(p * CAP, (p + 1) * CAP)
    lblk = lambda q, p: slice(4 * (q % 2) + p * BC, 4 * (q % 2) + (p + 1) * BC)
    slot = lambda c: c0 * CAP + 16 * c
    column = lambda b: BC * (cpos[b] - c0)
    half = [column(0), column(2)]
    pos = T.lst[:, 0:64]
    lst = lambda k, a, b: T.lst[:, 64 + (k - 1) * WC + a:64 + (k - 1) * WC + b]
    pa = [T.pa0, T.pa1]
    c16, kf, idc, dgc, n16 = [T.col[:, j:j + 1] for j in range(5)]
    own = column(r)
    land = BC if own == 0 else 0

    far = [q for q in peers if topo.die(T.cores[q]) != topo.die(core)]
    masks = {}
    for q in peers:
        en = topo.engines(core, T.cores[q])
        if q in far:
            j = far.index(q)
            pick = en[0::2][4 * j:4 * j + 4]
        else:
            pick = en[1::2][0:4]
        masks[q] = sum(1 << e for e in pick)

    def send(qs, src, dst, sem, local):
        def f(e):
            trs = []
            for q in qs:
                rid, pid, _ = topo.addr(T.cores[q])
                trs.append(RemoteDMATransfer(dst_ids=[DstId(rid=rid, pnc=pid)], dma_engine_mask=masks[q],
                                             remote_sem=T.sem[sem], src=src(q), dst=dst(q)))
            return e.remote_dma_fused(trs, local_sem=T.sem[local])
        return f

    op("a", dma(T.wcol[:, 0:1], T.wt[:]), wr=["wt"], sem="dwt")
    op("s", dma(T.c0[:], T.chunks[:]), wr=["c0"], sem="dch")
    op("a", dma(T.wide[:, 0:256], T.follow[:]), wr=["w0"], sem="dfo")
    op("s", dma(T.wide[:, 288:416], T.head[:]), wr=["w1"], sem="dhd")
    op("s", dma(T.wide[:, 256:288], T.vac[:]), wr=["w2"], sem="dva")
    op("s", dma(T.zw[:, 0:EARLY], T.store[:, 0:EARLY]), wr=["zv"], sem="dst")

    io = lambda out, pat, base, mult: (lambda e: e.iota(out, pat, base, mult, allow_small_or_imprecise_dtypes=True))
    keep = lambda out, in_, n, cmp, other, base, mult: (lambda e: e.affine_select(out, in_, [[-mult, n]], cmp, other, base, mult))
    op("g", lambda e: e.iota(T.ki[:, 0:1], [[0, 1]], 0, 1), wr=["k"])
    op("g", io(T.xi[:], [[1, 144]], -15, 0), wr=["xi"])
    op("g", io(T.e16[:], [[16, 8], [0, 16]], 0, 0), wr=["e16"])
    op("g", io(T.ind[:, 0::65], [[BC, N]], 0, 0), wr=["base"])
    op("g", io(kf, [[0, 1]], 0, 1), wr=["kf"])
    op("v", fill(T.cb[:, win], 0.0), wr=["win"])
    op("v", ts(T.ki[:, 1:2], T.ki[:, 0:1], 112, None, ALU.bitwise_and), rd=["k"], wr=["k112"])
    op("v", fill(T.rs2[:], 1.0), wr=["rs2"])
    op("v", cp(c16, T.ki[:, 1:2]), rd=["k112"], wr=["c16"])
    op("v", fill(T.rst[:], 1.0), wr=["rst"])
    op("v", ts(T.zwt[:], T.xi[:], c16, T.wcol[:, 0:1], ALU.is_equal, ALU.mult), rd=["xi", "c16", "wt"], wr=["zwt"])
    op("v", ts(T.bm[:], T.e16[:], c16, None, ALU.is_equal), rd=["e16", "c16"], wr=["bm"])
    op("v", fill(T.rs2[:, 0::65], 0.0), wr=["rs2"])
    op("v", fill(T.rst[:, 0::4], 0.0), wr=["rst"])
    op("g", keep(T.ud0[:], T.bm[:], 128, ALU.is_gt, 0.0, 0, -1), rd=["bm"], wr=["ud0"])
    op("g", keep(T.ud[:], T.ud0[:], 128, ALU.not_equal, BIG, 0, 1), rd=["ud0"], wr=["ud"])
    op("g", io(T.idlo[:], [[1, 256]], 0, 0), wr=["idlo"])
    W = N * CAP
    op("a", act(T.ft[:, 0:W], T.cb[:, win], ACT.Identity, bias=float(S * r)), rd=["win"], wr=["f0"])
    op("a", act(n16, c16, ACT.Identity, scale=-256.0), rd=["c16"], wr=["n16"])
    op("a", act(T.ft[:, W:2 * W], T.ft[:, 0:W], ACT.Copy), rd=["f0"], wr=["f1"])
    op("a", act(idc, kf, ACT.Identity, scale=256.0, bias=n16), rd=["kf", "n16"], wr=["idc"])
    op("a", act(T.z1[:], T.zwt[:], ACT.Sign), rd=["zwt"], wr=["z1"])
    op("a", act(T.ft[:, 2 * W:3 * W], T.ft[:, 0:W], ACT.Copy), rd=["f0"], wr=["f2"])
    op("a", act(T.idhi[:], T.idlo[:], ACT.Identity, bias=idc, scale=0.0), rd=["idlo", "idc"], wr=["idhi"])
    op("g", io(T.ft[:, 3 * W:S], [[0, S - 3 * W]], S * r, 0), wr=["f3"])

    op("p", fold(pa[0][:, 0:64], T.zwt, lambda i: T.c0[:, i::16]), rd=["zwt", "c0"], wr=["s"], bank=["pa0"])
    op("v", cp(T.whi[:, 0:256], T.wide[:, 0:256]), rd=["w0"], wr=["hi"])
    op("v", ts(T.t13[:, 0:64], pa[0][:, 0:64], 13.0, None, ALU.mult), rd=["s"], wr=["t13"], bank=["pa0"])
    op("v", ts(T.tb[:, 0:64], T.t13[:, 0:64], 2, N - 1, ALU.arith_shift_right, ALU.bitwise_and), rd=["t13"], wr=["tb"])
    qb = [slice(65 * j + 1, 65 * j + 65) for j in range(N)]
    for j in range(N):
        op("v", ts(T.ind[:, qb[j]], T.tb[:, 0:64], float(spos.index(w0 + j)), None, ALU.is_equal), rd=["tb"], wr=["ind%d" % j])
    op("v", scan(T.cum[:], T.rs2[:], T.ind[:], 0.0, ALU.add), rd=["rs2", "base"] + ["ind%d" % j for j in range(N)], wr=["cum"])
    op("p", pairs([(pa[1][:, j:256:4], T.bm, T.cum[:, 65 * j:65 * j + 64], T.ud, T.ind[:, qb[j]]) for j in range(N)]),
       rd=["bm", "ud", "cum"], wr=["pre"], bank=["pa1"])
    op("v", tt(T.wlo[:, 0:256], T.wide[:, 0:256], T.whi[:, 0:256], ALU.subtract), rd=["w0", "hi"], wr=["lo"])
    op("v", scan(T.mx[:], T.rst[:, 0:256], pa[1][:, 0:256], 0.0, ALU.max), rd=["pre", "rst"], wr=["mx"], bank=["pa1"])
    op("v", cp(T.hl[:], T.wide[:, 288:416]), rd=["w1"], wr=["hl"])
    op("v", ts(pos, T.mx[:, 3::4], -BIG, None, ALU.add), rd=["mx"], wr=["pos"])
    op("v", cp(T.cb[:, win].indirect(pos), T.c0[:]), rd=["pos", "c0"], wr=["win"])

    rows = [("a", T.ft[0::16, 0:S], T.whi[:, 0:256], "hi"), ("s", T.ft[1::16, 0:S], T.wlo[:, 0:256], "lo"),
            ("s", T.ft[3::16, 0:S], T.idlo[:], "idlo"), ("a", T.ft[2::16, 0:S], T.idhi[:], "idhi")]
    for j, (q, out, in_, key) in enumerate(rows):
        op(q, dma(out, in_), rd=["f0", "f1", "f2", "f3", key], wr=["ft%d" % j], sem="dft")
    op("s", dma(T.zw[:, EARLY:S], T.store[:, EARLY:S]), rd=["idhi"], wr=["zw"], sem="dst")
    ft = ["ft%d" % j for j in range(len(rows))]

    op("a", act(T.zs[:], T.z1[:], ACT.Identity, scale=PS), rd=["z1"], wr=["zs"])
    op("a", act(dgc, idc, ACT.Identity, scale=0.25 / UN, bias=S / UN), rd=["idc"], wr=["dgc"])
    op("a", act(T.nud[:], T.ud[:], ACT.Identity, scale=-1.0), rd=["ud"], wr=["nud"])
    op("g", keep(T.eye[:], T.bm[:], 128, ALU.is_equal, 0.0, 0, 1), rd=["bm"], wr=["eye"])
    op("g", keep(T.zf[:], T.zs[:], 144, ALU.is_ge, 0.0, -14, -1), rd=["zs"], wr=["zf"])
    op("g", keep(T.z2[:], T.zs[:], 144, ALU.is_ge, 0.0, 13, 1), rd=["zs"], wr=["z2"])
    op("g", keep(T.za[:], T.z2[:], 144, ALU.is_ge, 0.0, -12, -1), rd=["z2"], wr=["za"])
    op("a", act(T.neye[:], T.eye[:], ACT.Identity, scale=-1.0), rd=["eye"], wr=["neye"])
    op("a", act(T.dg[:], T.eye[:], ACT.Identity, scale=dgc), rd=["eye", "dgc"], wr=["dg"])

    op("g", send(peers, lambda q: T.cb[:, blk(spos[q])], lambda q: T.cb[:, blk(layout(q)[0][r])], "in", "sent0"),
       rd=["win"], wr=["sent0"], sem="sent0", n=4 * len(peers))
    op("p", fold(pa[0][:, 128:128 + WC], T.zwt, lambda i: T.cb[:, win.start + i:win.stop:16]), rd=["zwt", "win"], wr=["sw"], bank=["pa0"])
    op("v", fill(T.ft[:, S:FTW], float(S * r)), wr=["f4"])
    op("v", cp(T.whi[:, 256:288], T.wide[:, 256:288]), rd=["w2"], wr=["vhi"])
    op("v", fill(T.s2[:, 0:2], 64.0), wr=["s2-1"])
    op("v", tt(T.wlo[:, 256:288], T.wide[:, 256:288], T.whi[:, 256:288], ALU.subtract), rd=["w2", "vhi"], wr=["vlo"])
    op("v", ts(T.t13[:], pa[0][:, 128:128 + WC], 13.0, None, ALU.mult), rd=["sw"], wr=["t13"], bank=["pa0"])
    op("v", ts(T.tb[:], T.t13[:], 2032, None, ALU.bitwise_and), rd=["t13"], wr=["tb"])
    op("v", ts(T.tc[:], T.t13[:], 11, 15, ALU.arith_shift_right, ALU.bitwise_and), rd=["t13"], wr=["tc"])
    op("v", tt(T.td[:], T.tb[:], T.tc[:], ALU.add), rd=["tb", "tc"], wr=["td"])
    op("v", cp(T.lb[:, lblk(r, w0).start:lblk(r, w0 + N - 1).stop], T.td[:]), rd=["td"], wr=["lw"])
    op("g", send(peers, lambda q: T.lb[:, lblk(r, spos[q])], lambda q: T.lb[:, lblk(q, layout(q)[0][r])], "inl", "sentl"),
       rd=["lw"], wr=["sentL"], sem="sentl", n=4 * len(peers))
    op("s", dma(T.ft[2::16, S:FTW], T.whi[:, 256:288]), rd=["f4", "vhi", "sentL"], wr=["fv0"], sem="dfv")
    op("s", dma(T.ft[3::16, S:FTW], T.wlo[:, 256:288]), rd=["f4", "vlo"], wr=["fv1"], sem="dfv")
    op("g", keep(T.zy[:], T.z2[:], 144, ALU.is_ge, 0.0, -11, -1), rd=["z2"], wr=["zy"])
    op("v", fill(T.zw[:, S:ZWW], 0.0), wr=["spare"])
    op(None, None, wr=["in"], sem="in", n=4 * len(peers))
    op(None, None, wr=["inl"], sem="inl", n=4 * len(peers))

    op("a", scaled("a", T.ht[:, 0:16 * HA], T.ft[:, 0:S].indirect(T.hl[:, 0:HA]), -1.0 / PS), rd=ft + ["hl"], wr=["ht"])
    if HA < 128:
        op("v", scaled("v", T.ht[:, 16 * HA:B], T.ft[:, 0:S].indirect(T.hl[:, HA:128]), -1.0 / PS), rd=ft + ["hl"], wr=["hu"])
    ht = ["ht"] + ["hu"] * (HA < 128)

    def span(x):
        name, *part = str(x).split(":")
        a, n = {"o": (own, BC), "s": (column(r ^ 1), BC), "b": (half[1 - r // 2], HC), "r": (land, 3 * BC), "w": (0, WC),
                "0": (half[0], HC), "1": (half[1], HC)}[name]
        return (a + int(part[0]), a + int(part[1])) if part else (a, a + n)

    keys = lambda name, a, b: ["%s.%d" % (name, c) for c in range(a // GRAIN, b // GRAIN)]
    here = lambda a, b, mine="win", theirs="in": [mine] * (a < own + BC and b > own) + [theirs] * (a < own or b > own + BC)
    area = lambda j, a, b: T.pm[:, 2 * H * j + 16 * a:2 * H * j + 16 * b]
    px = lambda k, a, b: T[PX[k]][:, 128 * (k // 4) + a:128 * (k // 4) + b]

    def sums():
        op("p", fold(pa[1][:, 256 + land:256 + land + 3 * BC], T.zwt, lambda i: T.cb[:, slot(land) + i:slot(land + 3 * BC):16]),
           rd=["zwt", "in"], wr=["sr"], bank=["pa1"])

    def unused(x):
        a, b = span(x)
        name, at = ("pa0", 128 + (3 - w0) * BC) if x == "o" else ("pa1", 256 + a)
        op("a", act(T.inv[:, a:b], T[name][:, at:at + b - a], ACT.Relu, bias=UN, scale=-UN), rd=["sw" if x == "o" else "sr"],
           wr=keys("inv", a, b), bank=[name])

    def spare():
        op("p", pairs([(pa[1][:, 400:400 + WC], T.eye, T.idlo[:, 0:WC], T.eye, T.inv[:])]), rd=["eye", "idlo"] + keys("inv", 0, WC),
           wr=["sp"], bank=["pa1"])
        op("a", act(T.dmp[:], pa[1][:, 400:400 + WC], ACT.Relu, bias=-UN), rd=["sp"], wr=["dmp"], bank=["pa1"])

    def table(q, x):
        a, b = span(x)
        at = lblk(r, c0).start
        out, in_ = area(0, a, b), T.ht[:].indirect(T.lb[:, at + a:at + b])
        op(q, cp(out, in_) if q == "v" else act(out, in_, ACT.Copy), rd=ht + here(a, b, "lw", "inl"), wr=keys("t", a, b))

    def follow(q, k, x):
        a, b = span(x)
        op(q, scaled(q, area(k - 1, a, b), T.ft[:, 0:S].indirect(lst(k, a, b)), -1.0 / PS), rd=ft + keys("l%d" % k, a, b),
           wr=keys("p%d" % (k + 1), a, b))

    def chain(k, x):
        a, b = span(x)
        at = 2 * H * max(k - 2, 0)
        op("p", fold(px(k, a, b), T.za if k == 1 else T.zf, lambda i: T.pm[:, at + 16 * a + i:at + 16 * b:16]),
           rd=["za" if k == 1 else "zf"] + keys("t" if k < 3 else "p%d" % k, a, b), wr=keys("x%d" % k, a, b), bank=[PX[k]])

    def cvt(k, x):
        a, b = span(x)
        op("v", ts(lst(k, a, b), px(k, a, b), -1.0, None, ALU.mult), rd=keys("x%d" % k, a, b), wr=keys("l%d" % k, a, b), bank=[PX[k]])

    def compare(k, x):
        a, b = span(x)
        op("v", tt(area(2 + k, a, b), T.zw[:, 0:S].indirect(lst(k, a, b)), T.cb[:, slot(a):slot(b)], ALU.not_equal),
           rd=["zw"] + keys("l%d" % k, a, b) + here(a, b), wr=keys("m%d" % k, a, b))

    def minus(j, x):
        a, b = span(x)
        op("p", mm(T["pd%d" % j][:, 0:16 * (b - a)], T.neye[:], T.cb[:, slot(a):slot(b)], True, False), rd=["neye"] + here(a, b),
           wr=["df%d" % j], bank=["pd%d" % j])

    def pick(j, k, x):
        a, b = span(x)
        op("a", act(T.gs[:, 512 * j:512 * j + 16 * (b - a)], T.zw[:, 0:S].indirect(lst(k, a, b)), ACT.Copy),
           rd=["zw"] + keys("l%d" % k, a, b), wr=["gs%d" % j])

    def plus(j, x):
        a, b = span(x)
        op("p", mm(T["pd%d" % j][:, 0:16 * (b - a)], T.eye[:], T.gs[:, 512 * j:512 * j + 16 * (b - a)], False, True), rd=["eye", "gs%d" % j],
           wr=["df%d" % j], bank=["pd%d" % j])

    def size(j, k, x):
        a, b = span(x)
        op("a", act(area(2 + k, a, b), T["pd%d" % j][:, 0:16 * (b - a)], ACT.Abs), rd=["df%d" % j], wr=keys("m%d" % k, a, b), bank=["pd%d" % j])

    def differ(k, x):
        a, b = span(x)
        at = 2 * H * (2 + k)
        op("p", fold(T.pe[:, 4 * a + k - 1:4 * b:4], T.zs, lambda i: T.pm[:, at + 16 * a + i:at + 16 * b:16]),
           rd=["zs"] + keys("m%d" % k, a, b), wr=keys("e%d" % k, a, b), bank=["pe"])

    def side(k, x):
        a, b = span(x)
        op("a", act(T.pk[:, 4 * a + k - 1:4 * b:4], px(k, a, b), ACT.Copy), rd=keys("x%d" % k, a, b), wr=keys("k%d" % k, a, b), bank=[PX[k]])

    def found(x):
        a, b = span(x)
        c = slice(4 * a, 4 * b)
        op("v", tt(T.wk[:, c], T.pk[:, c], T.pe[:, c], ALU.add), rd=[y for k in ("k1", "k2", "k3", "k4", "e1", "e2", "e3", "e4") for y in keys(k, a, b)],
           wr=keys("wk", a, b), bank=["pe"])
        op("v", scan(T.mk[:, c], T.rst[:, 0:4 * (b - a)], T.wk[:, c], 0.0, ALU.min), rd=keys("wk", a, b) + ["rst"], wr=keys("mk", a, b))

    hit = lambda a, b: T.mk[:, 4 * a + 3:4 * b:4]

    def missed(x):
        a, b = span(x)
        op("v", tt(T.i2[:, a:b], hit(a, b), T.inv[:, a:b], ALU.is_ge), rd=keys("mk", a, b) + keys("inv", a, b), wr=keys("i2", a, b))

    def count(h):
        at, (a, b) = 2 + h * HC, span(h)
        op("v", scan(T.s2[:, at:at + HC], T.rs2[:, 1:1 + HC], T.i2[:, a:b], T.s2[:, at - 1:at], ALU.subtract),
           rd=keys("i2", a, b) + ["rs2", "s2%d" % (h - 1)], wr=["s2%d" % h])

    def rank(name, *hs):
        op("p", pairs([(T[name][:, 400 + half[h]:400 + half[h] + HC], T.bm, T.s2[:, 1 + h * HC:1 + (h + 1) * HC], T.nud,
                        T.i2[:, half[h]:half[h] + HC]) for h in hs]),
           rd=["bm", "nud"] + ["s2%d" % h for h in hs], wr=[k for h in hs for k in keys("q", *span(h))], bank=[name])

    def number(name, x):
        a, b = span(x)
        op("v", tt(T.ix[:, a:b], T[name][:, 400 + a:400 + b], hit(a, b), ALU.min), rd=keys("q", a, b), wr=keys("ix", a, b), bank=[name])
        op("v", ts(lst(5, a, b), T.ix[:, a:b], -1.0, None, ALU.mult), rd=keys("ix", a, b), wr=keys("l5", a, b))

    def answer(q, x):
        a, b = span(x)
        op(q, scaled(q, T.ab[:, slot(a):slot(b)], T.ft[:].indirect(lst(5, a, b)), 1.0 / PS),
           rd=ft + ["fv0", "fv1"] + keys("l5", a, b), wr=keys("ans", a, b))

    def reply(h):
        qs = [q for q in peers if q // 2 == h]
        op("g", send(qs, lambda q: T.ab[:, blk(cpos[q])], lambda q: T.ab[:, blk(layout(q)[1][r])], "back", "sent"),
           rd=[k for q in qs for k in keys("ans", column(q), column(q) + BC)], wr=["sent%d" % (h + 1)], sem="sent", n=4 * len(qs))

    def place(name, x):
        a, b = span(x)
        op("p", fold(T[name][:, 320 + a:320 + b], T.za, lambda i: T.ab[:, slot(a) + i:slot(b):16],
                     [(T.dg[:], T.inv[:, a:b]), (T.eye[:], T.dmp[:, a:b])]),
           rd=["za", "dg", "eye", "dmp"] + keys("ans", a, b), wr=keys("y", a, b), bank=[name])

    def target(name, x):
        a, b = span(x)
        op("v", cp(lst(6, a, b), T[name][:, 320 + a:320 + b]), rd=keys("y", a, b), wr=keys("l6", a, b), bank=[name])

    def put(x):
        a, b = span(x)
        op("v", cp(T.zw[:].indirect(lst(6, a, b)), T.cb[:, slot(a):slot(b)]), rd=keys("l6", a, b) + here(a, b), wr=["zw", "spare"])

    steps = {"sums": sums, "unused": unused, "table": table, "chain": chain, "cvt": cvt, "follow": follow, "compare": compare,
             "minus": minus, "pick": pick, "plus": plus, "size": size, "differ": differ, "side": side, "found": found,
             "missed": missed, "count": count, "rank": rank, "number": number, "answer": answer, "reply": reply, "spare": spare,
             "place": place, "target": target, "put": put}
    for line in PLAN[r // 2].split(","):
        name, *args = line.split()
        steps[name](*[int(x) if x.isdigit() else x for x in args])
    op("s", dma(T.z[:], T.zw[:, 0:S]), rd=["zw"], wr=["z"], sem="dz")

    op(None, None, wr=["back"], sem="back", n=4 * len(peers))
    op("a", act(T.yg[:], T.ab[:, win].indirect(pos), ACT.Copy), rd=["back", "pos"] + keys("ans", own, own + BC), wr=["yg"])
    op("p", fold(T.px2[:, 128:192], T.zy, lambda i: T.yg[:, 64 * i:64 * i + 64]), rd=["zy", "yg"], wr=["yp"], bank=["px2"])
    op("a", act(T.yo[:], T.px2[:, 128:192], ACT.Copy), rd=["yp"], wr=["yo"], bank=["px2"])
    op("a", dma(T.y[:], T.yo[:]), rd=["yo"], wr=["y"], sem="dy")
    op("a", None, rd=["y"])
    op("s", None, rd=["z"])
    op("g", None, rd=["sent0", "sentL", "sent1", "sent2"])
    emit(g, T, ops)


GRAIN = 10
PX = {1: "px1", 2: "px2", 3: "px3", 4: "px1"}
PLAN = 2 * ["""sums, table v 0:0:20, table a 0:20:40, table v 1:0:20, minus 0 1:20:40, chain 2 0, unused o, table a 1:20:40, cvt 2 0, chain 1 1, chain 2 1, compare 2 0:0:40, follow a 2 0, cvt 2 1, chain 1 0, compare 2 1:0:40, cvt 1 1, chain 3 0, follow a 2 1, cvt 3 0, cvt 1 0, differ 2 w, chain 3 1, side 2 w, follow a 3 0, chain 4 0, pick 0 1 1:20:40, compare 3 0:0:40, cvt 3 1, compare 1 0:0:40, plus 0 1:20:40, differ 3 0, cvt 4 0, follow a 3 1, compare 1 1:0:20, chain 4 1, size 0 1 1:20:40, side 3 0, side 4 0, compare 4 0:0:40, side 1 w, differ 1 w, cvt 4 1, unused r, differ 4 0, minus 1 1:20:40, pick 1 3 1:20:40, plus 1 1:20:40, side 3 1, pick 0 4 1:20:40, compare 3 1:0:20, found 0, minus 0 1:20:40, size 1 3 1:20:40, side 4 1, spare, plus 0 1:20:40, missed 0, size 0 4 1:20:40, count 0, rank px3 0, differ 3 1, compare 4 1:0:20, number px3 0, differ 4 1, answer a 0:20:40, answer v 0:0:20, found 1, place pa0 0, missed 1, count 1, target pa0 0, reply 0, rank px2 1, number px2 1, answer a 1, reply 1, put 0, place pa1 1, target pa1 1, put 1"""]
OLD = ["""unused o, table a w:40:80, table v w:0:40, chain 2 w, cvt 2 w, chain 1 w, follow a 2 w:30:80, follow v 2 w:0:30, sums, side 2 w,
    chain 3 w, cvt 1 w, compare 2 w, minus 0 w:50:80, pick 0 1 w:50:80, unused r, side 1 w, cvt 3 w, plus 0 w:50:80, follow a 3 w:20:80, follow v 3 w:0:20,
    differ 2 w, compare 1 w:0:50, size 0 1 w:50:80, chain 4 w, side 3 w, spare, minus 1 w:50:80, pick 1 3 w:50:80, compare 3 w:0:50, cvt 4 w,
    differ 1 w, plus 1 w:50:80, minus 0 w:50:80, pick 0 4 w:50:80, compare 4 w:0:50, size 1 3 w:50:80, plus 0 w:50:80, side 4 w,
    size 0 4 w:50:80, differ 3 w, differ 4 w, found w, missed w, count 0, count 1, rank px3 0 1, number px3 w, answer a 0:20:40, answer v 0:0:20,
    answer a 1, place pa0 0, reply 0, target pa0 0, put 0, place pa1 1, reply 1, target pa1 1, put 1"""]
